import numpy as np, ml_dtypes
CORES = [2,42,66,74,82,90,114]
N = 7
BF = ml_dtypes.bfloat16
def gentries(a):
    return np.ascontiguousarray(a.reshape(8, 16, -1).transpose(0, 2, 1)).reshape(8, -1)
def gtable(e):
    e = np.asarray(e); return np.ascontiguousarray(e.reshape(8, -1, 16).transpose(0, 2, 1)).reshape(128, -1).astype(np.int32)
V, FN, C, S, TV = 3072, 4096, 192, 745, 4
def perms(rng, *shape):
    return np.argsort(rng.random(shape), axis=-1)
def marks(rng, cnt):
    return np.argsort(rng.random(cnt.shape[:-2] + (16, cnt.shape[-1])), axis=-2) < cnt
def lay(loc, xw, nw, pw):
    inv = np.argsort(loc, axis=-1)
    x = np.take_along_axis(xw, inv[:, :, None, :], 3); nm = np.take_along_axis(nw, inv, 2)
    p = np.where(pw >= 0, np.take_along_axis(loc, np.maximum(pw, 0), 2), -1)
    return x, nm, p, np.take_along_axis(np.roll(loc, -1, axis=0), inv, 2)
def two(rng):
    return rng.integers(0, 64, (N, 16, FN)) + 192 * (np.arange(FN) & 1)
def reads(rng, hi):
    m = marks(rng, hi); return rng.integers(0, 64, m.shape) + 192 * m
def loose(rng, share):
    w = perms(rng, N, 8, FN); return np.where((w < V) & (rng.random((N, 8, FN)) < share), w, -1)
def tradition(rng):
    base = np.where(rng.random((8, 16, FN)) < 0.3, rng.choice(np.array([0, 128, 255]), (8, 16, FN)), rng.integers(0, 256, (8, 16, FN)))
    fo = np.where(rng.random((N, 8, 16, FN)) < 0.25, rng.integers(0, 256, (N, 8, 16, FN)), base)
    com = rng.integers(0, FN, (8, FN // 16))
    z = np.where(rng.random((8, V)) < 0.4, np.take_along_axis(com, rng.integers(0, FN // 16, (8, V)), 1), perms(rng, 8, FN)[:, :V])
    zz = np.where(rng.random((N, 8, V)) < 0.1, rng.integers(0, FN, (N, 8, V)), z)
    xw = np.take_along_axis(base[None], zz[:, :, None, :], 3)
    xw = np.where(rng.random((N, 8, 16, V)) < 0.25, rng.integers(0, 256, (N, 8, 16, V)), xw)
    nw = np.where(rng.random((N, 8, V)) < 0.15, rng.integers(0, FN, (N, 8, V)), z)
    pw = np.full((N, 8, FN), -1, np.int64); m = V // 12
    for r in range(N):
        for g in range(8):
            a = pw[r, g]; o = rng.permutation(V); a[z[g, o]] = o; a[rng.random(FN) < 0.3] = -1
            h = np.zeros(V, bool); h[a[a >= 0]] = True
            a[rng.permutation(np.flatnonzero(a < 0))[:m]] = rng.permutation(np.flatnonzero(~h))[:m]
    x, nm, p, cc = lay(perms(rng, N, 8, V), xw, nw, pw)
    for q in range(N):
        for g in range(8):
            i = rng.permutation(V)[:V // 32]; cc[q, g, i] = cc[q, g, rng.permutation(i)]
    return x, fo, nm, p, cc
def pack(x, fo, nm, p, cc):
    return {"tx": np.ascontiguousarray(x.reshape(N, 128, V)).astype(np.float32).astype(BF), "fo": np.ascontiguousarray(fo.reshape(N, 128, FN)).astype(np.float32).astype(BF),
            "nm": np.ascontiguousarray(nm).astype(np.int32), "pl": np.stack([gtable(a) for a in p]), "cc": np.stack([gtable(a) for a in cc])}
def setup_inputs(rng):
    return pack(*tradition(rng))
def setup_inputs_spread(rng):
    x = np.minimum(np.floor(256 * rng.random((N, 8, 16, V)) ** np.exp2(rng.integers(-2, 3, (N, 8, 1, V)))), 255)
    fo = np.minimum(np.floor(256 * rng.random((N, 8, 16, FN)) ** np.exp2(rng.integers(-2, 3, (N, 8, 1, FN)))), 255)
    nm = np.minimum(np.floor(FN * rng.random((N, 8, V)) ** np.exp2(rng.integers(-1, 3, (N, 8, 1)))), FN - 1)
    return pack(x, fo, nm, loose(rng, rng.choice(np.array([0.1, 0.3, 0.6, 1.0]), (N, 8, 1))), perms(rng, N, 8, V))
def setup_inputs_ends(rng):
    u = rng.integers(0, 2, (8, 16, 1)); side = rng.integers(0, 2, (8, 1, FN)); side[:, :, 0] = 0; side[:, :, FN - 1] = 1
    fl = rng.integers(1, 4, (N, 8, 1, FN)) * (rng.random((N, 8, 1, FN)) < 0.5); fl[..., 0] = 0; fl[..., FN - 1] = 0
    fo = 255 * (u ^ side ^ marks(rng, fl).astype(np.int64))
    xs = rng.integers(0, 2, (N, 8, 1, V)); xf = rng.choice(np.array([0, 1, 4, 7, 7, 8, 8, 16]), (N, 8, 1, V))
    e = np.arange(N)[:, None] + np.arange(8)[None, :]; v = np.array([0, 7, 8, 16])
    xs[..., 0] = 1; xs[..., V - 1] = 1; xf[:, :, 0, V - 1] = v[e & 3]; xf[:, :, 0, 0] = v[(e + 1) & 3]
    x = 255 * (u ^ xs ^ marks(rng, xf).astype(np.int64))
    nm = np.where(rng.random((N, 8, V)) < 0.7, (FN - 1) * rng.integers(0, 2, (N, 8, V)), rng.integers(0, FN, (N, 8, V))); nm[..., 0] = 0; nm[..., V - 1] = 0
    p = loose(rng, 0.4); p[(p == 0) | (p == V - 1)] = -1
    cc = np.zeros((N, 8, V), np.int64); cc[..., 1:V - 1] = 1 + perms(rng, N, 8, V - 2)
    for g in range(8):
        a, b = ((0, V - 1), (V - 1, 0))[g & 1]
        p[:, g, 0] = a; p[:, g, FN - 1] = b; cc[:, g, 0] = a; cc[:, g, V - 1] = b
    return pack(x, fo, nm, p, cc)
def hang(rng, un0):
    last = (S * TV - 1) % V; o = rng.permutation(V); o = np.concatenate([np.array([last]), o[o != last]]); un, on = o[:un0], o[un0:]
    phi = rng.permutation(FN)[:len(on)]; odd = phi[(phi & 1) == 1]; j = np.flatnonzero((phi & 1) == 0)[0]
    name = np.zeros(V, np.int64); name[on] = phi; name[un] = rng.choice(odd, un0); name[last] = phi[j]
    nm = np.tile(name, (N, 1)); q = rng.integers(0, N); nm[q, on[j]] = rng.choice(odd)
    hi = rng.choice(np.array([7, 8, 9]), (N, 1, V)); hi[q, 0, on[j]] = 8
    p = np.full(FN, -1, np.int64); p[phi] = on
    return reads(rng, hi), two(rng), nm, np.tile(p, (N, 1)), np.tile(np.arange(V), (N, 1))
def setup_inputs_corners(rng):
    x, fo, nm, p, cc = tradition(rng); o = rng.permutation(8)
    p[:, o[0]] = -1
    w = perms(rng, N, FN); p[:, o[1]] = np.where(w < V, w, -1)
    for r in range(N):
        w = rng.permutation(FN); a = np.where(w < V, w, -1)
        if r & 1: a[rng.choice(np.flatnonzero(a >= 0))] = -1
        else:
            a[:] = -1; a[rng.integers(0, FN)] = (0, V - 1)[(r >> 1) & 1]
        p[r, o[2]] = a
    for i in (3, 4):
        g = o[i]; fo[:, g] = two(rng); x[:, g] = reads(rng, rng.choice(np.array([0, 7, 7, 8, 8, 9, 9, 16]), (N, 1, V))); nm[:, g] = rng.integers(0, FN, (N, V))
        w = perms(rng, N, FN); p[:, g] = np.where((w < V) & ((i == 4) | (rng.random((N, FN)) < 0.5)), w, -1)
    cc[:, o[3]] = (np.arange(V) + 1) % V; cc[:, o[4]] = V - 1 - np.arange(V)
    for i, n in ((5, C - 2), (6, C - 1), (7, C)): x[:, o[i]], fo[:, o[i]], nm[:, o[i]], p[:, o[i]], cc[:, o[i]] = hang(rng, n)
    return pack(x, fo, nm, p, cc)
def late(rng, un0, vis, pair):
    n = len(vis)
    if pair: w = np.stack([rng.permutation(S)[:n], S * TV + rng.permutation(V - S * TV)[:n]])
    else: w = rng.permutation(V)[None, :n]
    o = rng.permutation(V); o = np.concatenate([w.reshape(-1), o[~np.isin(o, w)]]); un, on = o[:un0], o[un0:]
    a = rng.permutation(FN); new, phi = a[:n], a[FN - len(on):]; odd = phi[(phi & 1) == 1]
    name = np.zeros(V, np.int64); name[on] = phi; name[un] = rng.choice(odd, un0)
    nm = np.tile(name, (N, 1)); fo = two(rng); fo[:, :, new] = 255
    for k in range(n):
        r = int(rng.integers(0, N)); nm[(r + vis[k]) % N, w[:, k]] = new[k]; fo[r, :, int(new[k])] = rng.integers(0, 64, 16)
    hi = rng.choice(np.array([7, 8, 9]), (N, 1, V)); hi[:, :, w.reshape(-1)] = 0
    p = np.full(FN, -1, np.int64); p[phi] = on; x = reads(rng, hi)
    if pair: return x, fo, nm, np.tile(p, (N, 1)), np.tile(np.arange(V), (N, 1))
    x, nm, p, cc = lay(perms(rng, N, 1, V), x[:, None], nm[:, None], np.tile(p, (N, 1, 1)))
    return x[:, 0], fo, nm[:, 0], p[:, 0], cc[:, 0]
def turn(rng):
    c = rng.permutation(FN)[:N + 2]; x = rng.integers(0, 64, (N, 16, V)); fo = two(rng); fo[:, :, c] = 255
    nm = np.tile(c[:N, None], (1, V)); i = (S * TV + C) % V; nm[:, i - 1] = c[N]; nm[:, i] = c[N + 1]
    for r in range(N):
        t = 2 + r % (TV - 1); fo[r, :, int(c[(r + t) % N])] = rng.integers(0, 64, 16)
    return x, fo, nm, np.full((N, FN), -1, np.int64), np.tile(np.arange(V), (N, 1))
def setup_inputs_crowd(rng):
    x, fo, nm, p, cc = tradition(rng); o = rng.permutation(8); c = rng.permutation(FN)[:6 + N * TV]; half = loose(rng, 0.5)
    nm[:, o[0]] = c[0]; p[:, o[0]] = -1
    nm[:, o[1]] = c[1]; p[:, o[1]] = -1
    for t in range(1, TV + 1): nm[:, o[1], (S * t + 5) % V] = c[6 + N * (t - 1):6 + N * t]
    nm[:, o[2]] = c[2]; p[:, o[2]] = half[:, o[2]]
    nm[:, o[3]] = rng.choice(np.array([0, FN - 1, c[3]]), (N, V)); p[:, o[3]] = half[:, o[3]]
    nm[:, o[4]] = np.where((np.arange(V) & 1) == 1, c[3], c[4]); p[:, o[4]] = -1; p[1::2, o[4]] = half[1::2, o[4]]
    nm[:, o[5]] = c[5]; p[:, o[5]] = -1; p[:, o[5], c[5]] = V - 1
    x[:, o[6]], fo[:, o[6]], nm[:, o[6]], p[:, o[6]], cc[:, o[6]] = turn(rng)
    x[:, o[7]], fo[:, o[7]], nm[:, o[7]], p[:, o[7]], cc[:, o[7]] = late(rng, C // 2, list(range(1, TV + 1)), True)
    return pack(x, fo, nm, p, cc)
def still(rng, k):
    n = max(k - 1, 0); o = rng.permutation(V); un, on = o[:n], o[n:]
    phi = rng.permutation(FN)[:len(on)]; odd = phi[(phi & 1) == 1]; ev = on[(phi & 1) == 0]
    name = np.zeros(V, np.int64); name[on] = phi; name[un] = rng.choice(odd, n)
    nm = np.tile(name, (N, 1)); hi = rng.choice(np.array([7, 8, 9]), (N, 1, V))
    for q in range(N):
        w = ev[9 * q:9 * q + 9]; nm[q, w[1:]] = rng.choice(odd, 8); hi[q, 0, w[1:]] = rng.choice(np.array([7, 7, 6, 0]), 8)
        if k > 0 and q % 2 == 0:
            nm[q, w[0]] = rng.choice(odd); hi[q, 0, w[0]] = rng.choice(np.array([8, 8, 16]))
    p = np.full(FN, -1, np.int64); p[phi] = on
    x, nm, p, cc = lay(perms(rng, N, 1, V), reads(rng, hi)[:, None], nm[:, None], np.tile(p, (N, 1, 1)))
    return x[:, 0], two(rng), nm[:, 0], p[:, 0], cc[:, 0]
def setup_inputs_calm(rng):
    x, fo, nm, p, cc = tradition(rng); o = rng.permutation(8)
    for k in range(4): x[:, o[k]], fo[:, o[k]], nm[:, o[k]], p[:, o[k]], cc[:, o[k]] = still(rng, k)
    for k, n, vis, pair in ((4, 1, [2], False), (5, 1, [3], False), (6, 2 * TV, list(range(1, TV + 1)), True)):
        x[:, o[k]], fo[:, o[k]], nm[:, o[k]], p[:, o[k]], cc[:, o[k]] = late(rng, n, vis, pair)
    return pack(x, fo, nm, p, cc)
def check_inputs(d):
    bad = []
    for k, lo, hi in (("tx", 0, 255), ("fo", 0, 255), ("nm", 0, FN - 1), ("pl", -1, V - 1), ("cc", 0, V - 1)):
        v = np.asarray(d[k]).astype(np.float64)
        if not np.all((v >= lo) & (v <= hi) & (np.floor(v) == v)): bad.append("range of " + k)
    e = np.sort(np.stack([gentries(np.asarray(a)) for a in d["pl"]]), axis=-1)
    if np.any((e[..., 1:] == e[..., :-1]) & (e[..., 1:] >= 0)): bad.append("pl lists a place twice")
    e = np.sort(np.stack([gentries(np.asarray(a)) for a in d["cc"]]), axis=-1)
    if np.any(e != np.arange(V)): bad.append("cc is no permutation")
    return bad
def reference(tx, fo, nm, pl, cc):
    X = tx.astype(np.float32).astype(np.int32).reshape(N, 8, 16, V); F = fo.astype(np.float32).astype(np.int32).reshape(N, 8, 16, FN)
    name = nm.astype(np.int64).reshape(N, 8, V); P = np.stack([gentries(a) for a in pl]).astype(np.int64); con = np.stack([gentries(a) for a in cc]).astype(np.int64)
    forms = np.arange(FN)[None, :]
    for t in range(1, TV + 1):
        order = (np.arange(V) + S * t) % V
        for r in range(N):
            q = (r + t) % N; left = (r + t - 1) % N
            full = P[r] >= 0; y = np.where(full, np.take_along_axis(con[left], np.maximum(P[r], 0), 1), 0)
            n = np.take_along_axis(name[q], y, 1); x = np.take_along_axis(X[q], y[:, None, :], 2)
            near = np.abs(x - F[r]) < np.abs(x - np.take_along_axis(F[r], n[:, None, :], 2))
            votes = np.add.reduce(near.astype(np.int64), axis=1)
            other = full & (n != forms); amend = other & (votes >= 9)
            g, f = np.nonzero(amend); name[q, g, y[g, f]] = f
            p = np.where(full & ((n == forms) | amend), y, -1)
            listed = np.zeros((8, V), bool); g, f = np.nonzero(p >= 0); listed[g, p[g, f]] = True
            free = ~listed[:, order]; taken = free & (np.add.accumulate(free.astype(np.int64), axis=1) <= C)
            g, i = np.nonzero(taken); place = order[i]
            low = np.full((8, FN), V, np.int64); np.minimum.at(low, (g, name[q][g, place]), place)
            P[r] = np.where((p < 0) & (low < V), low, p)
    return {"yn": name.astype(np.float32), "yp": np.stack([gtable(a) for a in P]).astype(np.float32)}

@@ -1,0 +1,859 @@
+from concourse.mybir import AluOpType as Op, AxisListType, ActivationFunctionType as Act
+
+V, FN, C, STEP, TV = 3072, 4096, 192, 745, 4
+W = V // 16
+WF = FN // 16
+K = C // 16
+B0 = 64
+L1V = 144
+FINS = 160
+CH = 512
+NCH = V // CH
+TRV = 512
+DDW = 8 * K * (K + 1)
+WAW = max(V + 16 * L1V + 128, FN + V - 16 * FINS + C)
+WBW = max(V + 16 * (WF - L1V) + 128, FN + 16 * FINS)
+
+CYC, PEC, HOP, GATH, SCAT, SLIP = 0.00104, 0.00053, 0.08, 1.56, 3.8, 0.1
+
+f32, bf, i32, u16 = "float32", "bfloat16", "int32", "uint16"
+SCRATCH = {}
+
+
+def _sb(names, cols, dtype):
+    for n in names.split():
+        SCRATCH[n] = ("sbuf", [128, cols], dtype)
+
+
+_sb("XO X1 X2 X3 X4 WN WL FNB U", V, bf)
+_sb("F", B0 + FN, bf)
+_sb("TR", V + C, bf)
+_sb("PW1 PW2", B0 + FN + C, bf)
+_sb("WA", WAW, f32)
+_sb("WB", WBW, f32)
+_sb("IOF", FN, f32)
+_sb("SV CIW", V, f32)
+_sb("CCP CC1 CC2 IDT", 4 * W, bf)
+_sb("CC3", 2 * W, bf)
+_sb("CIU CI1 CI2 CI3 N0U N1 N2 N3 N4 NS1 NS2 NS3 LU CCU FOU", W, u16)
+_sb("PLU YU", WF, u16)
+_sb("PLI IA IB", WF, i32)
+_sb("CCI NMI IC ID", W, i32)
+_sb("IQ FA FB FC FD TA TB ZT YT YL YO", WF, f32)
+_sb("FE FG FH LF NF AB AD CUM STP TAU SD DMP FV TC", W, f32)
+_sb("NH NL LH LL DH DL FREE ALV CMA CMB CMC GN GC GP GI ZB KB E1 RR", W, bf)
+_sb("INV", WF, bf)
+_sb("RC", W + 16, bf)
+_sb("Z Z192 ZR", 144, bf)
+_sb("BO BO256 TRI I1 I2 IN1 IN2", 128, bf)
+_sb("IM IDF", 128, f32)
+_sb("PI", 16, i32)
+_sb("CF", 32, f32)
+_sb("SC", 16, f32)
+_sb("KT", 16 * 18, f32)
+_sb("KI", 32, i32)
+_sb("KH2 ZM", 32, bf)
+_sb("KU", 16 * 8, u16)
+_sb("BW", 16, f32)
+_sb("DD", DDW, f32)
+for _n in "S0 S1 S2 PV PC PA PB PK".split():
+    SCRATCH[_n] = ("psum", [128, 512], f32)
+PSUM = set("S0 S1 S2 PV PC PA PB PK".split())
+
+ND = 100
+ARR = ["ha", "hb", "hc", "ax0", "ax1", "ax2", "ax3", "ax4", "ac1", "ac2", "ac3", "ai1", "ai2", "ai3", "an1", "an2", "an3", "an4", "ay"]
+SEMAPHORES = ["cv", "cs", "cp", "cg", "sent"] + ARR + ["d%d" % i for i in range(ND)]
+
+
+ORDER = []
+ROUNDS = 100
+STEPS = 1200
+SPAN = []
+
+
+def order_calls(nodes):
+    m = len(nodes)
+    busy = [x["busy"] for x in nodes]
+    lat = [x["lat"] for x in nodes]
+    fwd = [[] for _ in range(m)]
+    bwd = [[] for _ in range(m)]
+    for k, x in enumerate(nodes):
+        for j, w in x["pre"].items():
+            lag = lat[j] + HOP if w else busy[j]
+            fwd[j].append((k, lag))
+            bwd[k].append((j, busy[k] + lag - busy[j]))
+
+    def place(edges, first, prio):
+        left = [0] * m
+        for i in range(m):
+            for k, _ in edges[i]:
+                left[k] += 1
+        ready = list(first)
+        start = [0.0] * m
+        taken = {}
+        can = [i for i in range(m) if left[i] == 0]
+        seq = []
+        while can:
+            i = min(can, key=lambda k: prio[k])
+            can.remove(i)
+            t0 = ready[i]
+            q = nodes[i]["q"]
+            if q is not None:
+                spans = taken.setdefault(q, [])
+                p = len(spans)
+                while p > 0 and spans[p - 1][1] > t0:
+                    p -= 1
+                while p < len(spans) and spans[p][0] < t0 + busy[i] - 1e-9:
+                    t0 = max(t0, spans[p][1])
+                    p += 1
+                spans.insert(p, (t0, t0 + busy[i]))
+            start[i] = t0
+            seq.append(i)
+            for k, lag in edges[i]:
+                ready[k] = max(ready[k], t0 + lag)
+                left[k] -= 1
+                if left[k] == 0:
+                    can.append(k)
+        return start, seq
+
+    seed = [12345]
+
+    def jitter(size):
+        out = []
+        for _ in range(m):
+            seed[0] = (seed[0] * 1103515245 + 12345) % 2147483648
+            out.append(size * seed[0] / 2147483648.0)
+        return out
+
+    best = None
+    prio = [float(i) for i in range(m)]
+    for r in range(ROUNDS):
+        start, seq = place(fwd, [0.0] * m, prio)
+        end = max(start[i] + lat[i] for i in range(m))
+        if best is None or end < best[0]:
+            best = (end, start, seq)
+        base = best[1] if r % 4 == 3 else start
+        noise = jitter(0.0 if r < 3 else (0.1, 0.3, 0.8)[r % 3])
+        back, _ = place(bwd, [lat[i] - busy[i] for i in range(m)],
+                        [float(noise[i]) - base[i] - busy[i] for i in range(m)])
+        noise = jitter(0.0 if r < 3 else (0.05, 0.2, 0.5, 1.0, 0.0)[r % 5])
+        prio = [float(noise[i]) - back[i] - busy[i] for i in range(m)]
+    for r in range(STEPS):
+        a = jitter(best[0])[0] - 4.0
+        noise = jitter((0.3, 0.8, 2.0)[r % 3])
+        prio = [best[1][i] + (noise[i] if a <= best[1][i] < a + 8.0 else 0.0) for i in range(m)]
+        start, seq = place(fwd, [0.0] * m, prio)
+        if r % 2:
+            back, _ = place(bwd, [lat[i] - busy[i] for i in range(m)], [-start[i] - busy[i] for i in range(m)])
+            start, seq = place(fwd, [0.0] * m, [-back[i] - busy[i] for i in range(m)])
+        end = max(start[i] + lat[i] for i in range(m))
+        if end <= best[0]:
+            best = (end, start, seq)
+    SPAN.append(best[0])
+    where = {i: p for p, i in enumerate(best[2])}
+    return sorted(range(m), key=lambda i: (best[1][i], where[i]))
+
+
+def helper(T, topo, r):
+    c, n = T.cores[r], len(T.cores)
+    for h in topo.cores_of(c):
+        if T.rank_of(h) is None and topo.die(h) != topo.die(c) and \
+                all(topo.may_write(h, T.cores[(r - t) % n]) for t in range(1, TV + 1)):
+            return h
+    raise ValueError("no helper core")
+
+
+def local_engines(T, topo, r):
+    far = topo.engines(T.cores[r], T.cores[(r - 1) % len(T.cores)])
+    return [e for e in topo.engines(T.cores[r], helper(T, topo, r)) if e not in far]
+
+
+def write(g, T, topo, out, src, sem, dst, engines):
+    mask = 0
+    for e in engines:
+        mask |= 1 << e
+    rid, pid = topo.addr(dst)[0], topo.addr(dst)[1]
+    g.remote_dma(out, src, T.sem[sem], T.sem.sent, pid, rid, mask)
+
+
+def helper_program(g, core, r, T, topo):
+    n = len(T.cores)
+    m = len(local_engines(T, topo, r))
+    sent = 0
+    plan = [("hb", T.X1[:, V // 2:V], T.XO[:, V // 2:V], "ax1", 1), ("hc", T.CC1[:, :], T.CCP[:, :], "ac1", 1),
+            ("ha", T.X2[:, :], T.XO[:, :], "ax2", 2), (None, T.CC2[:, :], T.CCP[:, :], "ac2", 2),
+            (None, T.X3[:, :], T.XO[:, :], "ax3", 3), (None, T.CC3[:, :], T.CCP[:, 0:2 * W], "ac3", 3),
+            (None, T.X4[:, :], T.XO[:, :], "ax4", 4)]
+    for need, out, src, sem, t in plan:
+        if need:
+            g.wait_ge(T.sem[need], m)
+        dst = T.cores[(r - t) % n]
+        e = topo.engines(core, dst)
+        write(g, T, topo, out, src, sem, dst, e)
+        sent += len(e)
+    g.wait_ge(T.sem.sent, sent)
+
+
+def rank_program(g, core, T, topo):
+    rank = T.rank_of(core)
+    n = len(T.cores)
+    if rank is None:
+        for r in range(n):
+            if helper(T, topo, r) == core:
+                helper_program(g, core, r, T, topo)
+        return
+    Q = {"v": g.vector, "s": g.scalar, "p": g.tensor, "g": g, "y": g.sync}
+    CS = {"v": "cv", "s": "cs", "p": "cp", "g": "cg"}
+    cnt = {}
+    waited = {}
+    hist = {}
+    nd = [0]
+
+    def A(b, lo=0, hi=None, st=1, parts=None):
+        if hi is None:
+            hi = SCRATCH[b][1][1]
+        ps = slice(0, 128) if parts is None else slice(0, parts)
+        ap = T[b][ps, lo:hi] if st == 1 else T[b][ps, lo:hi:st]
+        return (b, ap, lo, hi, None)
+
+    def ROW(b, r, lo, hi):
+        return (b, T[b][r:128:16, lo:hi], lo, hi, r)
+
+    def IND(win, off):
+        return (win[0], win[1].indirect(off[1]), win[2], win[3], None, off)
+
+    def col(b, j):
+        return A(b, j, j + 1)
+
+    def wait(q, tok):
+        s, v = tok
+        if waited.get((q, s), 0) < v:
+            Q[q].wait_ge(T.sem[s], v)
+            waited[(q, s)] = v
+
+    nodes = []
+
+    def node(q, kind, fn, reads, writes, busy, lat, cont=False):
+        me = len(nodes)
+        pre = {}
+        for x, wr in [(r, False) for r in reads] + [(w, True) for w in writes]:
+            b, lo, hi, row = x[0], x[2], x[3], x[4]
+            ps = b in PSUM
+            for (l2, h2, r2, w2, j) in hist.get(b, []):
+                apart = h2 <= lo or hi <= l2 or (row is not None and r2 is not None and row != r2)
+                same = kind == "c" and nodes[j]["kind"] == "c" and nodes[j]["q"] == q
+                if same and q == "p" and ps:
+                    pre[j] = pre.get(j, False) or (not apart and not cont)
+                elif ((w2 or wr) and not apart) or (ps and not same):
+                    pre[j] = True
+        for x, wr in [(r, False) for r in reads] + [(w, True) for w in writes]:
+            h = hist.setdefault(x[0], [])
+            if wr and x[4] is None and not cont:
+                h[:] = [e for e in h if not (x[2] <= e[0] and e[1] <= x[3] and e[4] in pre)]
+            h.append((x[2], x[3], x[4], wr, me))
+        nodes.append({"q": q, "kind": kind, "fn": fn, "pre": pre, "busy": busy, "lat": lat})
+        return me
+
+    def width(x):
+        if len(x) > 5:
+            return 16 * (x[5][3] - x[5][2])
+        return x[3] - x[2]
+
+    def cost(q, out, ins, per):
+        ops = [x for x in ins if isinstance(x, tuple)]
+        m = max(width(x) for x in [out] + ops[:1])
+        if len(out) > 5:
+            m, per = width(out), SCAT
+        elif ops and len(ops[0]) > 5:
+            per = GATH
+        elif per is None:
+            narrow = all(SCRATCH[x[0]][2] in (bf, u16) for x in [out] + ops if x[3] - x[2] > 1)
+            per = 0.5 if narrow else 1.0
+        return {"v": 0.05, "s": 0.065, "g": 0.15}[q] + max(64, m * per) * CYC
+
+    def emit():
+        tok = {}
+        if not ORDER:
+            ORDER.extend(order_calls(nodes))
+        for i in ORDER:
+            x = nodes[i]
+            if x["kind"] == "arr":
+                tok[i] = x["fn"]
+                continue
+            best = {}
+            for j, w in x["pre"].items():
+                if w:
+                    s, v = tok[j]
+                    best[s] = max(best.get(s, 0), v)
+            for s, v in best.items():
+                wait(x["q"], (s, v))
+            ins = x["fn"]()
+            if x["kind"] == "c":
+                s = CS[x["q"]]
+                cnt[s] = cnt.get(s, 0) + 1
+                ins.then_inc(T.sem[s], 1)
+                tok[i] = (s, cnt[s])
+            elif x["kind"] == "dma":
+                s = "d%d" % nd[0]
+                nd[0] += 1
+                cnt[s] = 16
+                ins.then_inc(T.sem[s], 16)
+                tok[i] = (s, 16)
+        for s in sorted(cnt):
+            wait("g", (s, cnt[s]))
+
+    def split(ops):
+        out = []
+        for x in ops:
+            if isinstance(x, tuple):
+                out.append(x)
+                if len(x) > 5:
+                    out.append(x[5])
+        return out
+
+    def ap(x):
+        return x[1] if isinstance(x, tuple) else x
+
+    def run(q, fn, out, ins, per=None):
+        reads = split(ins) + ([out[5]] if len(out) > 5 else [])
+        d = cost(q, out, ins, per)
+        node(q, "c", fn, reads, [out], d, d)
+
+    def ts(out, in0, s1, op0, s2=None, op1=None):
+        if op1 is None:
+            run("v", lambda: g.vector.tensor_scalar(ap(out), ap(in0), ap(s1), None, op0), out, [in0, s1])
+        else:
+            run("v", lambda: g.vector.tensor_scalar(ap(out), ap(in0), ap(s1), ap(s2), op0, op1), out, [in0, s1, s2])
+
+    def tt(out, a, b, op):
+        run("v", lambda: g.vector.tensor_tensor(ap(out), ap(a), ap(b), op), out, [a, b],
+            1.0 if a[0] in PSUM or b[0] in PSUM else 2.0)
+
+    def cp(out, a):
+        run("v", lambda: g.vector.tensor_copy(ap(out), ap(a)), out, [a])
+
+    def fill(out, c):
+        run("v", lambda: g.vector.memset(ap(out), c), out, [])
+
+    def act(out, a, func=Act.Identity, bias=None, scale=None, per=1.0):
+        kw = {}
+        if bias is not None:
+            kw["bias"] = ap(bias)
+        if scale is not None:
+            kw["scale"] = ap(scale)
+        run("s", lambda: g.scalar.activation(ap(out), ap(a), func, **kw), out, [a, bias, scale], per)
+
+    def mm(out, terms, first=True, last=True):
+        def fn():
+            ins = None
+            for i, (l, r) in enumerate(terms):
+                ins = g.tensor.matmul(out[1], l[1], r[1], first and i == 0, last and i == len(terms) - 1)
+            return ins
+        d = sum(max(64, out[3] - out[2]) * (4 if SCRATCH[l[0]][2] == f32 else 1) * PEC for l, r in terms)
+        node("p", "c", fn, [x for t in terms for x in t], [out], d, d + 0.06, cont=not first)
+
+    def ext(out, b, lo, hi, z="Z", more=()):
+        mm(out, [(A(z, 15 - i, 143 - i), A(b, lo + i, hi, 16)) for i in range(16)], last=not more)
+        if more:
+            mm(out, list(more), first=False)
+
+    def dma(out, src, q="y", after=None):
+        reads = ([src] if isinstance(src, tuple) else []) + ([after] if after else [])
+        writes = [out] if isinstance(out, tuple) else []
+        x = out if writes else src
+        big = x[4] is None and x[3] - x[2] >= V
+        node(q, "dma", lambda: Q[q].dma_start(ap(out), ap(src)), reads, writes, 0.1,
+             (13.0 if SCRATCH[x[0]][2] == f32 else 7.0) if big else 2.5)
+
+    arrival = {}
+
+    def post(src, land, sem, dst, e, opens):
+        cnt["sent"] = cnt.get("sent", 0) + len(e)
+        i = node("g", "send", lambda: write(g, T, topo, land[1], src[1], sem, dst, e), [src], [], 0.3, 0.3)
+        for s in opens:
+            nodes[arrival[s]]["pre"][i] = True
+
+    def send(src, land, sem, k):
+        dst = T.cores[(rank + k) % n]
+        post(src, land, sem, dst, topo.engines(core, dst), [sem])
+
+    def hand(src, sem):
+        opens = {"hb": ["ax1"], "hc": ["ac1", "ac2", "ac3"], "ha": ["ax2", "ax3", "ax4"]}[sem]
+        post(src, src, sem, helper(T, topo, rank), local_engines(T, topo, rank), opens)
+
+    def expect(land, sem, src):
+        cnt[sem] = len(topo.engines(src, core))
+        lat = {"ax0": 18.0, "ax1": 21.0, "ac1": 20.0, "ax2": 28.0, "ac2": 32.0, "ax3": 42.0, "ac3": 45.0, "ax4": 56.0,
+               "ay": 5.0}.get(sem, 3.8)
+        arrival[sem] = node(None, "arr", (sem, cnt[sem]), [], [land], lat, lat)
+
+    for t in range(1, TV + 1):
+        far = helper(T, topo, (rank + t) % n)
+        if t == 1:
+            expect(A("X1", 0, V // 2), "ax0", T.cores[(rank + 1) % n])
+            expect(A("X1", V // 2, V), "ax1", far)
+        else:
+            expect(A("X%d" % t), "ax%d" % t, far)
+        expect(A("N%d" % t), "an%d" % t, T.cores[(rank + 1) % n])
+        if t < TV:
+            expect(A("CC%d" % t), "ac%d" % t, far)
+            expect(A("CI%d" % t), "ai%d" % t, T.cores[(rank + t) % n])
+    expect(A("YL"), "ay", T.cores[(rank - TV) % n])
+
+    def hilo(hi, lo, x):
+        cp(hi, x)
+        tt(lo, x, hi, Op.subtract)
+
+    def sigma(out, xi, ti, tf, tf2, w):
+        ts(ti, xi, 4, Op.arith_shift_right)
+        ts(tf, xi, float(w), Op.mult)
+        ts(tf2, ti, float(1 - 16 * w), Op.mult)
+        tt(out, tf, tf2, Op.add)
+
+    def iota(out, pat, base, cm, fl=True):
+        if fl:
+            run("g", lambda: g.iota(ap(out), pat, base, cm, allow_small_or_imprecise_dtypes=True), out, [], 2.0)
+        else:
+            run("g", lambda: g.iota(ap(out), pat, base, cm), out, [])
+
+    PF, PM, PG, PH, ZC, R12, LO1, PW_, RM, R0 = 0, 1, 2, 3, 4, 5, 6, 7, 8, 16
+
+    def rm(pair):
+        return col("CF", RM + pair)
+
+    dma(A("CCI"), T.cc[:, :], "y")
+    dma(A("PLI"), T.pl[:, :], "s")
+    dma(A("NMI"), T.nm[:, :], "s")
+    dma(A("XO"), T.tx[:, :], "y")
+    iota(A("IQ"), [[1, WF]], 0, 0)
+    iota(col("PI", 0), [[1, 1]], 0, 1, False)
+    iota(A("IM"), [[1, 8], [0, 16]], 0, 0)
+    iota(A("IOF", 0, FN // 2), [[1, FN // 2]], B0, 0)
+    for i in range(16):
+        sv = A("SV", i, V, 16)
+        act((sv[0], sv[1], 0, V, i), A("IQ", 0, W), bias=float(W * i + B0), per=1.0 / 16)
+    fill(A("WL"), 0.0)
+    fill(A("ZT"), 0.0)
+    ts(col("PI", 1), col("PI", 0), 15, Op.bitwise_and)
+    ts(col("PI", 2), col("PI", 0), 4, Op.arith_shift_right)
+    ts(col("PI", 3), col("PI", 0), 15, Op.bitwise_and, 1, Op.arith_shift_right)
+    cp(A("CF", 0, 4), A("PI", 0, 4))
+
+    ts(A("IC"), A("CCI"), 15, Op.bitwise_and)
+    ts(A("ID"), A("CCI"), 4, Op.arith_shift_right)
+    ts(A("CCP", 2 * W, 3 * W), A("IC"), float(W), Op.mult)
+    cp(A("CCP", 3 * W, 4 * W), A("ID"))
+    dma(ROW("WL", 4, 0, V), A("CCP", 2 * W, 3 * W), "y")
+    dma(ROW("WL", 5, 0, V), A("CCP", 3 * W, 4 * W), "y")
+    tt(A("FE"), A("CCP", 2 * W, 3 * W), A("CCP", 3 * W, 4 * W), Op.add)
+    ts(A("FG"), A("NMI"), float(B0), Op.add)
+    cp(A("CCU"), A("FE"))
+    act(A("CCP", 0, W), A("CCP", 3 * W, 4 * W), scale=16.0)
+    act(A("CCP", W, 2 * W), A("CCP", 2 * W, 3 * W), scale=1.0 / W)
+    def scatter(q, win, off, lo, hi, vals, step=32):
+        for a in range(lo, hi, step):
+            b = min(hi, a + step)
+            if q == "v":
+                cp(IND(A(win), A(off, a, b)), A(vals, 16 * a, 16 * b))
+            else:
+                act(IND(A(win), A(off, a, b)), A(vals, 16 * a, 16 * b), Act.Silu)
+
+    scatter("s", "CIW", "CCU", 0, W, "SV", 64)
+    hilo(A("NH"), A("NL"), A("FG"))
+    dma(ROW("WL", 0, 0, V), A("NH"), "y")
+    dma(ROW("WL", 1, 0, V), A("NL"), "y")
+    for b in ("WA", "WB"):
+        dma(ROW(b, 0, 0, V), A("ZT", 0, W), "y")
+    hand(A("XO", V // 2, V), "hb")
+    send(A("XO", 0, V // 2), A("X1", 0, V // 2), "ax0", -1)
+    hand(A("CCP"), "hc")
+    hand(A("XO", 0, V // 2), "ha")
+    iota(A("FD", 0, L1V), [[16, L1V]], V, 1)
+    iota(A("FD", L1V, WF), [[16, WF - L1V]], V, 1)
+    iota(A("IOF", FN // 2, FN), [[1, FN // 2]], B0 + FN // 2, 0)
+    sigma(A("FA"), A("PLI"), A("IA"), A("FB"), A("FC"), W)
+    ts(col("CF", ZC), col("CF", PG), 16.0, Op.mult, 15.0, Op.add)
+    ts(A("CF", RM, RM + 8), A("IQ", 0, 8), col("CF", PH), Op.is_equal)
+    cp(A("PLU"), A("FA"))
+    dma(A("F", B0, B0 + FN), T.fo[:, :], "y", A("PLU"))
+    dma(A("F", 0, B0), T.fo[:, 0:B0], "y", A("PLU"))
+    dma(A("PW1", 0, B0), T.fo[:, 0:B0], "y", A("PLU"))
+    for h in range(4):
+        lo, hi = h * WF // 4, (h + 1) * WF // 4
+        ts(A("PW1", B0 + 16 * lo, B0 + 16 * hi), IND(A("WL"), A("PLU", lo, hi)), rm(2), Op.mult)
+        if h == 0:
+            ts(A("Z"), A("IQ", 0, 144), col("CF", ZC), Op.is_equal)
+            ts(A("I1"), A("IQ", 0, 128), col("CF", PF), Op.is_equal)
+            ts(A("INV"), A("PLI"), 0.0, Op.is_lt, 8192.0, Op.mult)
+            ts(A("ZR"), A("IQ", 0, 144), col("CF", ZC), Op.is_equal, col("CF", RM), Op.mult)
+        ext(A("PC" if h < 3 else "PA", lo, hi), "PW1", B0 + 16 * lo, B0 + 16 * hi, more=[(A("I1"), A("INV", lo, hi))])
+        if h == 1:
+            ext(A("PV", 0, W), "WL", 0, V, "ZR")
+    tt(A("FA", 0, W), A("PC", 0, W), A("FD", 0, W), Op.min)
+    cp(A("N0U"), A("PV", 0, W))
+    send(A("N0U"), A("N1"), "an1", -1)
+    tt(A("FA", W, WF), A("PA", W, WF), A("FD", W, WF), Op.min)
+    cp(A("YU"), A("FA"))
+    dma(A("TC"), ROW("CIW", 0, 0, V), "y")
+    act(IND(A("WB"), A("YU", L1V, WF)), A("IOF", 16 * L1V, FN), Act.Silu)
+    cp(IND(A("WA"), A("YU", 0, L1V)), A("IOF", 0, 16 * L1V))
+    dma(A("TA", 0, W), ROW("WA", 0, 0, V), "y")
+    dma(A("TB", 0, W), ROW("WB", 0, 0, V), "s")
+    ts(A("CIU"), A("TC"), B0 - 0.25, Op.subtract)
+    for t in (1, 2, 3):
+        send(A("CIU"), A("CI%d" % t), "ai%d" % t, -t)
+    ts(A("I2"), A("IQ", 0, 128), col("CF", PF), Op.is_equal, 2.0, Op.mult)
+    ts(A("IN2"), A("IQ", 0, 128), col("CF", PF), Op.is_equal, -2.0, Op.mult)
+    ts(A("IN1"), A("IQ", 0, 128), col("CF", PF), Op.is_equal, -1.0, Op.mult)
+    ts(A("IDF"), A("IQ", 0, 128), col("CF", PF), Op.is_equal)
+    ts(A("BO"), A("IM"), col("CF", PG), Op.is_equal)
+    run("g", lambda: g.affine_select(T.TRI[:, :], T.BO[:, :], [[1, 128]], Op.is_ge, 0.0, 0, -1), A("TRI"), [A("BO")])
+    fill(A("ZB"), 0.0)
+    fill(A("RC", 0, 1), 0.0)
+    fill(A("YT"), 0.0)
+    ts(col("CF", PW_), col("CF", PM), float(W), Op.mult)
+
+    def fn_gather(t, c):
+        act(A("FNB", c * CH, (c + 1) * CH), IND(A("F"), A("N%d" % t, c * CH // 16, (c + 1) * CH // 16)))
+
+    for c in range(NCH):
+        fn_gather(1, c)
+    cp(A("NF"), A("N1"))
+    tt(A("FE"), A("TA", 0, W), A("TB", 0, W), Op.add)
+    ts(A("LU"), A("FE"), 0.25, Op.add)
+    dma(A("WA", 0, FN), A("IOF"), "y", A("LU"))
+    for b in ("WA", "WB"):
+        dma(ROW(b, 0, 0, FN), A("ZT"), "y")
+    dma(A("WN"), T.tx[:, :], "y", A("YU"))
+    dma(A("PW2", 0, FN), T.fo[:, :], "y", A("LU"))
+    dma(A("PW2", FN, FN + B0), T.fo[:, 0:B0], "y", A("LU"))
+
+    def kt(j):
+        return A("KT", 16 * j, 16 * j + K)
+
+    def ku(j):
+        return A("KU", 16 * j, 16 * j + K)
+    KW, KH, DTR, DPW, VAL, DFI, T1V, NW, NM_, DM, T1, T2, K1, K2, K3, K4, K5 = [kt(j) for j in range(17)]
+    A16, CWB = A("KH2", 0, K), A("KH2", 16, 16 + K)
+
+    def late_constants(c):
+        if c == 0:
+            act(A("KB"), A("IQ", 0, W))
+            act(A("IDT", W, 2 * W), A("IQ", 0, W))
+            act(A("IDT", 0, W), A("ZB"), bias=col("CF", PW_))
+            act(A("IDT", 2 * W, 3 * W), A("IQ", 0, W), scale=16.0)
+            act(A("IDT", 3 * W, 4 * W), A("ZB"), bias=col("CF", PM))
+            for r in range(4):
+                dma(ROW("WN", r, 0, V), A("IDT", r * W, (r + 1) * W), "y")
+            for r in range(2):
+                dma(ROW("PW2", r, 0, V), A("ZB"), "y")
+                dma(ROW("PW2", r, V, FN + B0), A("ZB", 0, (FN + B0 - V) // 16), "y")
+            ts(KW, A("IQ", 0, K), 16.0, Op.mult, col("CF", PM), Op.add)
+            ts(col("CF", R12), col("CF", PM), float(K - 1), Op.is_lt)
+            ts(col("CF", LO1), col("CF", PM), 1.0, Op.is_equal)
+            ts(col("CF", R0), col("CF", PM), 0.0, Op.is_equal)
+        if c == 1:
+            ts(A("BO256"), A("IM"), col("CF", PG), Op.is_equal, 256.0, Op.mult)
+            ts(A("Z192"), A("IQ", 0, 144), col("CF", ZC), Op.is_equal, float(W), Op.mult)
+            for t in range(1, TV + 1):
+                ts(col("ZM", t), col("CF", PM), float((STEP * t) % V % 16), Op.is_lt)
+        if c == 2:
+            act(KH, KW, bias=-0.5, scale=0.5)
+            act(DTR, KW, bias=float(V))
+            act(DPW, KW, bias=float(B0 + FN))
+            act(DFI, KW, bias=float(FN + V - 16 * FINS))
+
+    LQ = 64
+
+    def pre_ops(t, c):
+        if c == 0:
+            if t == 1:
+                cp(A("LF"), A("LU"))
+            else:
+                cp(A("LU", LQ, W), A("PA", 0, W - LQ))
+                act(A("LF", 0, LQ), A("PC", 0, LQ))
+                act(A("LF", LQ, W), A("PA", 0, W - LQ))
+            act(A("NH"), A("NF"))
+            act(A("LH"), A("LF"))
+            mm(A("PA", 0, W), [(A("IDF"), A("NF")), (A("IN1"), A("NH"))])
+            mm(A("PC", W, 2 * W), [(A("IDF"), A("LF")), (A("IN1"), A("LH"))])
+            mm(A("PC", 0, W), [(A("I1"), A("LH"))])
+            act(A("RR"), A("LH"), Act.Relu, bias=float(B0), scale=-1.0)
+            act(A("NL"), A("PA", 0, W))
+            act(A("LL"), A("PC", W, 2 * W))
+        if c == 1:
+            mm(A("PK", 0, W), [(A("I1"), A("LH")), (A("I1"), A("LL")), (A("IN1"), A("NH")), (A("IN1"), A("NL"))])
+            dma(ROW("WN", 4, 0, V), A("NH"), "y")
+            dma(ROW("WN", 5, 0, V), A("NL"), "y")
+            if t < TV:
+                for r in range(4 if t < 3 else 2):
+                    dma(ROW("WN", 2 + 4 * t + r, 0, V), A("CC%d" % t, r * W, (r + 1) * W), "y")
+            act(A("AB"), A("PK", 0, W), Act.Abs)
+            act(A("E1"), A("AB"), Act.Relu, bias=100.0, scale=-100.0)
+        if c == 2 and t == TV:
+            ts(A("IC"), A("LF"), float(B0), Op.subtract)
+            act(A("DMP", 0, FINS), A("IQ", 0, FINS), bias=col("CF", PM), scale=16.0)
+            act(A("DMP", FINS, W), A("IQ", 0, W - FINS), bias=col("CF", PM), scale=16.0)
+            act(A("DMP"), A("DMP"), bias=float(FN))
+            act(A("FG"), A("LF"), bias=float(-B0 * WF), scale=float(WF))
+            ts(A("ID"), A("IC"), 4, Op.arith_shift_right)
+            act(A("FH"), A("DMP"), scale=-1.0)
+        if c == 3 and t == TV:
+            ts(A("FE"), A("ID"), float(1 - FN), Op.mult)
+            mm(A("PB", 0, W), [(A("IDF"), A("FE")), (A("IDF"), A("FG")), (A("IDF"), A("FH"))])
+            act(A("SD"), A("PB", 0, W))
+
+    def judge(t):
+        x = "X%d" % t
+        sb = ["S0", "S1", "S2"]
+
+        def rg(c):
+            return c * CH, (c + 1) * CH
+
+        def listed(c):
+            return IND(A("F"), A("LU", c * CH // 16, (c + 1) * CH // 16))
+
+        bank = {0: "S0", 1: "S1", 2: "S2", 3: "PA", 4: "S1", 5: "S0"}
+
+        def u(c):
+            r = rg(c)
+            mm(A(bank[c]), [(A("IN2"), A(x, *r)), (A("I2"), A("FNB", *r))], last=False)
+            tt(A("U", *r), listed(c), A("FNB", *r), Op.subtract)
+            mm(A(bank[c]), [(A("I1"), A("U", *r))], first=False)
+
+        def u_scalar(c):
+            r = rg(c)
+            mm(A("PB"), [(A("I1"), A("U", *r)), (A("IN1"), A("FNB", *r))])
+            mm(A(bank[c]), [(A("IN2"), A(x, *r)), (A("I1"), A("FNB", *r)), (A("I1"), A("U", *r))])
+            act(A("U", *r), A("PB"), Act.Sign)
+
+        def prod(c, own=False):
+            r = rg(c)
+            tt(A("U", *r), A(bank[c]), A("U", *r), Op.mult)
+            if own:
+                ts(A("U", *r), A("U", *r), 0.0, Op.is_ge, 0.5, Op.subtract)
+            else:
+                act(A("U", *r), A("U", *r), Act.Sign, bias=0.5)
+
+        def votes(c0, c1):
+            lo, hi = c0 * CH, c1 * CH
+            a, b = lo // 16, hi // 16
+            mm(A("PV", a, b), [(A("IN1"), A("E1", a, b)), (A("I1"), A("RR", a, b))], last=False)
+            mm(A("PV", a, b), [(A("Z", 15 - i, 143 - i), A("U", lo + i, hi, 16)) for i in range(16)], first=False)
+
+        def more(c):
+            pre_ops(t, c)
+            if t == 1:
+                late_constants(c)
+
+        u(0)
+        more(0)
+        u(1)
+        act(A("U", *rg(3)), listed(3))
+        prod(0)
+        u(2)
+        u_scalar(3)
+        more(1)
+        act(A("U", *rg(4)), listed(4))
+        prod(1)
+        u(5)
+        u_scalar(4)
+        more(2)
+        prod(2)
+        votes(0, 2)
+        more(3)
+        prod(3, True)
+        votes(2, 4)
+        prod(5, True)
+        prod(4, True)
+        votes(4, 6)
+
+    def look(buf, win, off, pair, out):
+        ts(A(buf), IND(win, off), rm(pair), Op.mult)
+        ext(out, buf, 0, W)
+
+    def recount(t):
+        s = (STEP * t) % V
+        sc = s // 16
+        last = t == TV
+        pa, pb = A("PA", 0, K), A("PB", 0, K)
+        ts(A("FREE"), A("PV", 0, W), 0.0, Op.is_ge)
+        act(A("ALV"), A("FREE"), bias=1.0, scale=-1.0)
+        run("v", lambda: g.vector.tensor_tensor_scan(T.RC[:, 1:W + 1], T.FREE[:, :], T.ZB[:, :], 0.0, Op.add, Op.add),
+            A("RC", 1, W + 1), [A("FREE"), A("ZB")])
+        ts(col("RC", W + 1), col("FREE", sc), col("ZM", t), Op.mult, col("RC", sc), Op.add)
+        mm(A("S2", 0, 2), [(A("BO"), A("RC", W, W + 2))])
+        mm(A("S1", 0, 1), [(A("Z", 15 - i, 143 - i), col("RC", 16 * i + 16)) for i in range(K)])
+        mm(pb, [(A("Z", 15 - i, 143 - i), A("RC", i + 1, W + 1, 16)) for i in range(16)])
+        mm(A("S0", 0, W), [(A("BO"), A("RC", 0, W)), (A("TRI"), A("FREE"))])
+        if not last:
+            tt(A("DH"), A("PC", 0, W), A("ALV"), Op.mult)
+            tt(A("DL"), A("PC", W, 2 * W), A("ALV"), Op.mult)
+            dma(ROW("WL", 4, 0, V), A("DH"), "y")
+            dma(ROW("WL", 5, 0, V), A("DL"), "y")
+        else:
+            tt(A("PV", 0, W), A("ALV"), A("SD"), Op.mult)
+            tt(A("FG"), A("PV", 0, W), A("DMP"), Op.add)
+            cp(A("FOU"), A("FG"))
+        act(A("BW", 0, K), pb)
+        act(A("CUM"), A("S0", 0, W))
+        if last:
+            scatter("s", "WB", "FOU", 0, FINS, "IOF", 16)
+            scatter("v", "WA", "FOU", FINS, W, "IOF", 8)
+        else:
+            for lo in range(0, V - TRV, CH):
+                hi = min(lo + CH, V - TRV)
+                act(A("TR", lo, hi), IND(A("WL"), A("CI%d" % t, lo // 16, hi // 16)), scale=rm(2))
+            for lo in range(V - TRV, V, 256):
+                ts(A("TR", lo, lo + 256), IND(A("WL"), A("CI%d" % t, lo // 16, lo // 16 + 16)), rm(2), Op.mult)
+        tot, cs = col("S2", 0), col("S2", 1)
+        base = A("PV", 256, 256 + W)
+        ts(col("SC", 0), tot, float(C), Op.subtract, cs, Op.min)
+        ts(col("SC", 1), col("SC", 0), 0.0, Op.max)
+        ts(col("SC", 2), col("SC", 1), -1.0, Op.mult, cs, Op.add)
+        ts(base, A("IQ", 0, W), col("SC", 2), Op.is_ge, col("SC", 1), Op.mult)
+        tt(A("TAU"), base, A("IQ", 0, W), Op.add)
+        ts(A("CMA"), A("TAU"), col("S1", 0), Op.is_ge, col("CF", R12), Op.mult)
+        ext(pa, "CMA", 0, W)
+        ts(VAL, KW, tot, Op.is_lt)
+        tt(A("AD"), A("PK", 0, W), A("ALV"), Op.mult)
+        mm(A("S2", 0, W), [(A("I1"), A("NH")), (A("I1"), A("NL")), (A("IDF"), A("AD"))])
+        cp(ku(0), pa)
+        tt(A("CMB"), IND(A("BW", 0, K), ku(0)), A("TAU"), Op.is_le)
+        ts(A16, pa, 16.0, Op.mult)
+        ext(pb, "CMB", 0, W, more=[(A("I1"), A16)])
+        if not last:
+            cp(A("NS%d" % t), A("S2", 0, W))
+            send(A("NS%d" % t), A("N%d" % (t + 1)), "an%d" % (t + 1), -1)
+        else:
+            ts(A("FH"), A("S2", 0, W), float(B0), Op.subtract)
+        ts(ku(1), pb, float(W - 1), Op.min)
+        tt(A("CMC"), IND(A("CUM"), ku(1)), A("TAU"), Op.is_le)
+        cp(CWB, pb)
+        ext(pa, "CMC", 0, W, "Z192", more=[(A("I1"), CWB)])
+        if t in (2, 3):
+            cp(IND(A("PW%d" % (t - 1)), ku(5)), A("GI"))
+        if last:
+            for gi in range(8):
+                for h in range(2):
+                    mm(A("S0", 32 * gi + 16 * h, 32 * gi + 16 * h + 16, parts=W // 2),
+                       [(A("FH", h, W, 2), A("IDF", 16 * gi, 16 * gi + 16))])
+        ts(ku(2), pa, float(V - 1), Op.min)
+        ts(A("GN"), IND(A("WN"), ku(2)), rm(2), Op.mult)
+        ext(pb, "GN", 0, W)
+        mm(A("PK", 0, W), [(A("BO256"), A("GN")), (A("I1"), A("KB"))])
+        if not last:
+            look("GC", A("WN"), ku(2), 1 + 2 * t, pa)
+            cp(ku(3), pb)
+        else:
+            ts(A("GC"), IND(A("WN"), ku(2)), rm(1), Op.mult)
+            mm(A("PC", 0, W), [(A("BO"), A("GC"))])
+        ts(K2, pb, -256.0, Op.mult)
+        cp(NW, pb)
+        tt(NM_, K2, KH, Op.subtract)
+        if not last:
+            cp(A("GP"), IND(A("PW1", 0, B0 + FN), ku(3)))
+            ext(pb, "GP", 0, W)
+        seg = []
+        o = 0
+        for j in range(K):
+            w = 16 * (j + 1)
+            seg.append(A("DD", o, o + w))
+            o += w
+            act(seg[j], A("PK", 0, w), bias=col("KT", 16 * 8 + j))
+        red = [0]
+
+        def reduce(m):
+            for j in range(red[0], min(K, red[0] + m)):
+                out = col("KT", 16 * 9 + j)
+                run("v", lambda j=j, out=out: g.vector.tensor_reduce(out[1], seg[j][1], AxisListType.X, Op.min,
+                                                                     apply_absolute_value=True), out, [seg[j]])
+            red[0] = min(K, red[0] + m)
+
+        if last:
+            dma(A("TB"), ROW("WB", 0, 0, FN), "s")
+            cp(A("YT", 0, WF, parts=W // 2), A("S0", 0, WF, parts=W // 2))
+            send(A("YT"), A("YL"), "ay", TV)
+            ts(A("KI", 0, K), NW, float(B0), Op.subtract)
+            ts(A("FV"), A("PC", 0, W), float(B0), Op.add)
+            sigma(K3, A("KI", 0, K), A("KI", 16, 16 + K), K1, K2, WF)
+            reduce(4)
+            tt(T1, K3, DFI, Op.subtract)
+            reduce(4)
+            cp(ku(3), K3)
+            ts(A("GP"), IND(A("WA", 0, FN), ku(3)), 1.0, Op.is_lt, col("CF", R0), Op.mult)
+            ext(pb, "GP", 0, W)
+            tt(T2, T1, VAL, Op.mult)
+            tt(T1V, pb, T2, Op.mult)
+            reduce(K)
+            tt(K1, DM, KH, Op.is_gt)
+            tt(K2, T1V, K1, Op.mult)
+            tt(K4, K2, DFI, Op.add)
+            cp(ku(4), K4)
+            cp(IND(A("WA"), ku(4)), A("FV"))
+            dma(A("TA"), ROW("WA", 0, 0, FN), "y")
+            ts(A("PA", 0, WF), A("TB"), 1.0, Op.is_lt)
+            ts(A("IA"), A("TB"), float(B0), Op.subtract)
+            tt(A("PB", 0, WF), A("PA", 0, WF), A("TA"), Op.mult)
+            tt(A("FC"), A("PB", 0, WF), A("IA"), Op.add)
+            ts(A("YO"), A("FC"), -1.0, Op.max)
+            for gi in range(8):
+                dma(T.yn[gi, :], A("YL", 32 * gi, 32 * gi + 32, parts=W // 2), "s")
+            dma(T.yp[:, :], A("YO"), "y")
+            return
+        if t == 1:
+            act(A("GI"), IND(A("WN"), ku(2)), scale=rm(0))
+        if t == 2:
+            act(A("GI"), IND(A("WN"), ku(2)), scale=rm(0), bias=col("CF", LO1))
+        for c in range(NCH):
+            fn_gather(t + 1, c)
+        tt(T1, pa, DTR, Op.subtract)
+        if t == 3:
+            look("GI", A("PW2", 0, B0 + FN), ku(3), 0, pa)
+        reduce(3)
+        cp(ku(4), pb)
+        pos = ku(4)
+        if t >= 2:
+            look("GP", A("WN"), pos, 4, pb)
+            if t == 3:
+                ts(K1, pa, 0.5, Op.is_lt)
+                ts(K2, pa, 1.0, Op.subtract, 0.0, Op.max)
+                reduce(2)
+                tt(K3, pb, K1, Op.mult)
+                tt(K4, K3, K2, Op.add)
+                cp(ku(5), K4)
+                look("GP", A("WN"), ku(5), 6, pb)
+            reduce(4)
+            cp(ku(6), pb)
+            pos = ku(6)
+        look("GP", A("WL"), pos, 2, pb)
+        tt(T1V, T1, VAL, Op.mult)
+        reduce(3)
+        tt(K2, pb, NW, Op.not_equal)
+        reduce(1)
+        tt(K3, K2, T1V, Op.mult)
+        reduce(K)
+        tt(K1, DM, KH, Op.is_gt)
+        tt(K4, K1, K3, Op.mult)
+        tt(K5, K4, DTR, Op.add)
+        cp(ku(7), K5)
+        cp(IND(A("TR"), ku(7)), A("GN"))
+        ext(A("PC", 0, LQ), "TR", 0, 16 * LQ)
+        ext(A("PA", 0, W - LQ), "TR", 16 * LQ, V)
+        if t < 3:
+            tt(T2, NW, DPW, Op.subtract)
+            tt(K3, K2, VAL, Op.mult)
+            tt(K4, K1, T2, Op.mult)
+            cp(A("NF"), A("N%d" % (t + 1)))
+            tt(K5, K4, K3, Op.mult)
+            cp(A("LU", 0, LQ), A("PC", 0, LQ))
+            tt(K4, K5, DPW, Op.add)
+            cp(ku(5), K4)
+        else:
+            cp(A("NF"), A("N%d" % (t + 1)))
+            cp(A("LU", 0, LQ), A("PC", 0, LQ))
+
+    for t in range(1, TV + 1):
+        judge(t)
+        recount(t)
+    emit()

@@ -2,19 +2,26 @@ from concourse.mybir import AluOpType as Op, AxisListType, ActivationFunctionTyp
 
 V, FN, C, STEP, TV = 3072, 4096, 192, 745, 4
 W = V // 16
+WS = W + 16
+VS = 16 * WS
 WF = FN // 16
 K = C // 16
-B0 = 64
-L1V = 144
-FINS = 160
+B0 = 256
+BI = 64
+DEAD = 8192.0
+OUT = 16384.0
+FB = 512
 CH = 512
 NCH = V // CH
+L1V = 176
+YV = 256
+FINS = 144
 TRV = 512
-DDW = 8 * K * (K + 1)
-WAW = max(V + 16 * L1V + 128, FN + V - 16 * FINS + C)
-WBW = max(V + 16 * (WF - L1V) + 128, FN + 16 * FINS)
+FNV = 0
+KIND = "AEAEAB"
+LQ = 64
 
-CYC, PEC, HOP, GATH, SCAT, SLIP = 0.00104, 0.00053, 0.08, 1.56, 3.8, 0.1
+CYC, PEC, HOP, GATH, SCAT = 0.0009, 0.00045, 0.08, 1.56, 3.8
 
 f32, bf, i32, u16 = "float32", "bfloat16", "int32", "uint16"
 SCRATCH = {}
@@ -25,43 +32,51 @@ def _sb(names, cols, dtype):
         SCRATCH[n] = ("sbuf", [128, cols], dtype)
 
 
-_sb("XO X1 X2 X3 X4 WN WL FNB U", V, bf)
-_sb("F", B0 + FN, bf)
-_sb("TR", V + C, bf)
-_sb("PW1 PW2", B0 + FN + C, bf)
-_sb("WA", WAW, f32)
-_sb("WB", WBW, f32)
+_sb("XO X1 X2 X3 X4 FNB U AQ", V, bf)
+_sb("WN WL", VS, bf)
+_sb("F PW", B0 + FN, bf)
+_sb("TR", V + 256, bf)
+_sb("WA WB", FB + FN, f32)
 _sb("IOF", FN, f32)
-_sb("SV CIW", V, f32)
-_sb("CCP CC1 CC2 IDT", 4 * W, bf)
-_sb("CC3", 2 * W, bf)
-_sb("CIU CI1 CI2 CI3 N0U N1 N2 N3 N4 NS1 NS2 NS3 LU CCU FOU", W, u16)
+_sb("SV", V, f32)
+_sb("CIW", VS, f32)
+_sb("CCP CC1 CC2 IDT", 4 * WS, bf)
+_sb("CC3 CIH CH1 LHL", 2 * WS, bf)
+_sb("MS MR", 2 * WS * TV, bf)
+_sb("NS NR", W * TV, u16)
+_sb("CIU CI1 CI2 CI3 LU CCU FOU", W, u16)
 _sb("PLU YU", WF, u16)
-_sb("PLI IA IB", WF, i32)
-_sb("CCI NMI IC ID", W, i32)
-_sb("IQ FA FB FC FD TA TB ZT YT YL YO", WF, f32)
-_sb("FE FG FH LF NF AB AD CUM STP TAU SD DMP FV TC", W, f32)
-_sb("NH NL LH LL DH DL FREE ALV CMA CMB CMC GN GC GP GI ZB KB E1 RR", W, bf)
-_sb("INV", WF, bf)
-_sb("RC", W + 16, bf)
-_sb("Z Z192 ZR", 144, bf)
-_sb("BO BO256 TRI I1 I2 IN1 IN2", 128, bf)
+_sb("PLI IA", WF, i32)
+_sb("CCI NMI", W, i32)
+_sb("IC ID", WS, i32)
+_sb("FA FC FD TA TB ZT YT YL YO", WF, f32)
+_sb("FE FG FH TAU DMP FV FP", W, f32)
+_sb("CUM TC", WS, f32)
+_sb("NH NL THR CMA CMB CMC GP GL KEEP KV", W, bf)
+_sb("G1", 2 * W, bf)
+_sb("FREE ZB", WS, bf)
+_sb("IQ INV", WF, bf)
+_sb("RC", WS + 16, bf)
+_sb("EB", K * W, bf)
+_sb("ZZ", 10 * 144, bf)
+_sb("MM", 10 * 128, bf)
+_sb("TD", 16 * 128, bf)
 _sb("IM IDF", 128, f32)
 _sb("PI", 16, i32)
 _sb("CF", 32, f32)
+_sb("CB", 16, bf)
 _sb("SC", 16, f32)
-_sb("KT", 16 * 18, f32)
-_sb("KI", 32, i32)
-_sb("KH2 ZM", 32, bf)
-_sb("KU", 16 * 8, u16)
+_sb("KT", 16 * 10, f32)
+_sb("KI", 16, i32)
+_sb("KU", 16 * 10, u16)
 _sb("BW", 16, f32)
-_sb("DD", DDW, f32)
-for _n in "S0 S1 S2 PV PC PA PB PK".split():
+PSUM = "J0 J1 J2 K0 K1 PV PD PL".split()
+for _n in PSUM:
     SCRATCH[_n] = ("psum", [128, 512], f32)
-PSUM = set("S0 S1 S2 PV PC PA PB PK".split())
 
 ND = 100
-ARR = ["ha", "hb", "hc", "ax0", "ax1", "ax2", "ax3", "ax4", "ac1", "ac2", "ac3", "ai1", "ai2", "ai3", "an1", "an2", "an3", "an4", "ay"]
+ARR = ["ha", "hb", "hc", "ax0", "ax1", "ax2", "ax3", "ax4", "ac1", "ac2", "ac3", "ai1", "ai2", "ai3", "ah",
+       "an1", "an2", "an3", "an4", "am1", "am2", "am3", "am4", "ay"]
 SEMAPHORES = ["cv", "cs", "cp", "cg", "sent"] + ARR + ["d%d" % i for i in range(ND)]
 
 
@@ -182,7 +197,7 @@ def helper_program(g, core, r, T, topo):
     sent = 0
     plan = [("hb", T.X1[:, V // 2:V], T.XO[:, V // 2:V], "ax1", 1), ("hc", T.CC1[:, :], T.CCP[:, :], "ac1", 1),
             ("ha", T.X2[:, :], T.XO[:, :], "ax2", 2), (None, T.CC2[:, :], T.CCP[:, :], "ac2", 2),
-            (None, T.X3[:, :], T.XO[:, :], "ax3", 3), (None, T.CC3[:, :], T.CCP[:, 0:2 * W], "ac3", 3),
+            (None, T.X3[:, :], T.XO[:, :], "ax3", 3), (None, T.CC3[:, :], T.CCP[:, 0:2 * WS], "ac3", 3),
             (None, T.X4[:, :], T.XO[:, :], "ax4", 4)]
     for need, out, src, sem, t in plan:
         if need:
@@ -265,7 +280,7 @@ def rank_program(g, core, T, topo):
         if len(out) > 5:
             m, per = width(out), SCAT
         elif ops and len(ops[0]) > 5:
-            per = GATH
+            m, per = width(out), GATH
         elif per is None:
             narrow = all(SCRATCH[x[0]][2] in (bf, u16) for x in [out] + ops if x[3] - x[2] > 1)
             per = 0.5 if narrow else 1.0
@@ -335,35 +350,48 @@ def rank_program(g, core, T, topo):
     def fill(out, c):
         run("v", lambda: g.vector.memset(ap(out), c), out, [])
 
-    def act(out, a, func=Act.Identity, bias=None, scale=None, per=1.0):
+    def act(out, a, func=Act.Identity, bias=None, scale=None):
         kw = {}
         if bias is not None:
             kw["bias"] = ap(bias)
         if scale is not None:
             kw["scale"] = ap(scale)
-        run("s", lambda: g.scalar.activation(ap(out), ap(a), func, **kw), out, [a, bias, scale], per)
+        run("s", lambda: g.scalar.activation(ap(out), ap(a), func, **kw), out, [a, bias, scale], 1.0)
 
     def mm(out, terms, first=True, last=True):
         def fn():
             ins = None
-            for i, (l, r) in enumerate(terms):
-                ins = g.tensor.matmul(out[1], l[1], r[1], first and i == 0, last and i == len(terms) - 1)
+            for i, x in enumerate(terms):
+                o = x[2] if len(x) > 2 else out
+                ins = g.tensor.matmul(o[1], x[0][1], x[1][1], first and i == 0, last and i == len(terms) - 1)
             return ins
-        d = sum(max(64, out[3] - out[2]) * (4 if SCRATCH[l[0]][2] == f32 else 1) * PEC for l, r in terms)
-        node("p", "c", fn, [x for t in terms for x in t], [out], d, d + 0.06, cont=not first)
+        d = sum(max(64, x[1][1].shape[1]) * (4 if SCRATCH[x[0][0]][2] == f32 else 1) * PEC for x in terms)
+        node("p", "c", fn, [y for x in terms for y in x[:2]], [out], d, d + 0.06, cont=not first)
 
-    def ext(out, b, lo, hi, z="Z", more=()):
-        mm(out, [(A(z, 15 - i, 143 - i), A(b, lo + i, hi, 16)) for i in range(16)], last=not more)
-        if more:
-            mm(out, list(more), first=False)
+    ZALL, Z16, ZWS, Z01, ZL, ZN0, Z45, Z67, Z89, ZAB = range(10)
+    I1, I2, IN1, IN2, I256, INB, BO, TRI, BO45 = [A("MM", 128 * j, 128 * j + 128) for j in range(9)]
+    IDF = A("IDF")
+
+    def TDm(i):
+        return A("TD", 128 * i, 128 * i + 128)
+
+    def zs(z, i):
+        return A("ZZ", 144 * z + 15 - i, 144 * z + 143 - i)
+
+    def ext(out, b, lo, hi, z=ZALL, first=True, last=True):
+        mm(out, [(zs(z, i), A(b, lo + i, hi, 16)) for i in range(16)], first, last)
 
     def dma(out, src, q="y", after=None):
         reads = ([src] if isinstance(src, tuple) else []) + ([after] if after else [])
         writes = [out] if isinstance(out, tuple) else []
         x = out if writes else src
         big = x[4] is None and x[3] - x[2] >= V
-        node(q, "dma", lambda: Q[q].dma_start(ap(out), ap(src)), reads, writes, 0.1,
-             (13.0 if SCRATCH[x[0]][2] == f32 else 7.0) if big else 2.5)
+        node(q, "dma", lambda: Q[q].dma_start(ap(out), ap(src)), reads, writes, 0.07,
+             (11.0 if SCRATCH[x[0]][2] == f32 else 6.0) if big else 2.3)
+
+    def rows(win, r, b, lo, m=2):
+        for j in range(m):
+            dma(ROW(win, r + j, 0, VS), A(b, lo + j * WS, lo + (j + 1) * WS))
 
     arrival = {}
 
@@ -383,476 +411,411 @@ def rank_program(g, core, T, topo):
 
     def expect(land, sem, src):
         cnt[sem] = len(topo.engines(src, core))
-        lat = {"ax0": 18.0, "ax1": 21.0, "ac1": 20.0, "ax2": 28.0, "ac2": 32.0, "ax3": 42.0, "ac3": 45.0, "ax4": 56.0,
-               "ay": 5.0}.get(sem, 3.8)
+        lat = {"ax0": 13.0, "ax1": 15.0, "ac1": 15.0, "ax2": 24.0, "ac2": 27.0, "ax3": 36.0, "ac3": 39.0, "ax4": 48.0,
+               "ay": 4.5}.get(sem, 3.3)
         arrival[sem] = node(None, "arr", (sem, cnt[sem]), [], [land], lat, lat)
 
+    def names(b, t):
+        return A(b, W * t, W * t + W)
+
+    def halves(b, t, h=None):
+        if h is None:
+            return A(b, 2 * WS * t, 2 * WS * (t + 1))
+        return A(b, (2 * t + h) * WS, (2 * t + h) * WS + W)
+
+    nxt = T.cores[(rank + 1) % n]
     for t in range(1, TV + 1):
         far = helper(T, topo, (rank + t) % n)
         if t == 1:
-            expect(A("X1", 0, V // 2), "ax0", T.cores[(rank + 1) % n])
+            expect(A("X1", 0, V // 2), "ax0", nxt)
             expect(A("X1", V // 2, V), "ax1", far)
         else:
             expect(A("X%d" % t), "ax%d" % t, far)
-        expect(A("N%d" % t), "an%d" % t, T.cores[(rank + 1) % n])
+        expect(names("NR", t - 1), "an%d" % t, nxt)
+        expect(halves("MR", t - 1), "am%d" % t, nxt)
         if t < TV:
             expect(A("CC%d" % t), "ac%d" % t, far)
             expect(A("CI%d" % t), "ai%d" % t, T.cores[(rank + t) % n])
+    expect(A("CH1"), "ah", nxt)
     expect(A("YL"), "ay", T.cores[(rank - TV) % n])
 
-    def hilo(hi, lo, x):
-        cp(hi, x)
-        tt(lo, x, hi, Op.subtract)
-
-    def sigma(out, xi, ti, tf, tf2, w):
-        ts(ti, xi, 4, Op.arith_shift_right)
-        ts(tf, xi, float(w), Op.mult)
-        ts(tf2, ti, float(1 - 16 * w), Op.mult)
-        tt(out, tf, tf2, Op.add)
-
-    def iota(out, pat, base, cm, fl=True):
-        if fl:
-            run("g", lambda: g.iota(ap(out), pat, base, cm, allow_small_or_imprecise_dtypes=True), out, [], 2.0)
+    def iota(out, pat, base, cm):
+        if SCRATCH[out[0]][2] == i32:
+            run("g", lambda: g.iota(ap(out), pat, base, cm), out, [], 2.0)
         else:
-            run("g", lambda: g.iota(ap(out), pat, base, cm), out, [])
+            run("g", lambda: g.iota(ap(out), pat, base, cm, allow_small_or_imprecise_dtypes=True), out, [], 2.0)
 
-    PF, PM, PG, PH, ZC, R12, LO1, PW_, RM, R0 = 0, 1, 2, 3, 4, 5, 6, 7, 8, 16
+    def pick(out, src, pat, base):
+        run("g", lambda: g.affine_select(ap(out), ap(src), pat, Op.is_ge, 0.0, base, -1), out, [src], 2.0)
 
-    def rm(pair):
-        return col("CF", RM + pair)
+    def gather(q, out, win, off):
+        if q == "v":
+            cp(out, IND(win, off))
+        else:
+            act(out, IND(win, off))
+
+    def scatter(q, win, off, lo, hi, vals, step):
+        for a in range(lo, hi, step):
+            b = min(hi, a + step)
+            if q == "v":
+                cp(IND(win, A(off, a, b)), A(vals, 16 * a, 16 * b))
+            else:
+                act(IND(win, A(off, a, b)), A(vals, 16 * a, 16 * b), Act.Silu)
+
+    def pass_names(t, ps):
+        cp(names("NS", t), ps)
+        send(names("NS", t), names("NR", t), "an%d" % (t + 1), -1)
+        act(halves("MS", t, 0), ps)
+        tt(halves("MS", t, 1), ps, halves("MS", t, 0), Op.subtract)
+        send(halves("MS", t), halves("MR", t), "am%d" % (t + 1), -1)
+
+    PF, PM, PG, PH, ZC, R12, PW_, RL, R4, RD, RM = 0, 1, 2, 3, 4, 5, 6, 7, 16, 17, 8
+    LH, LL = A("LHL", 0, W), A("LHL", WS, WS + W)
+
+    def cf(j):
+        return col("CF", j)
+
+    def zmat(z, w=None):
+        if w is None:
+            ts(A("ZZ", 144 * z, 144 * z + 144), A("IQ", 0, 144), cf(ZC), Op.is_equal)
+        else:
+            ts(A("ZZ", 144 * z, 144 * z + 144), A("IQ", 0, 144), cf(ZC), Op.is_equal, w, Op.mult)
+
+    def diag(out, w):
+        ts(out, A("IQ", 0, 128), cf(PF), Op.is_equal, w, Op.mult)
 
     dma(A("CCI"), T.cc[:, :], "y")
     dma(A("PLI"), T.pl[:, :], "s")
     dma(A("NMI"), T.nm[:, :], "s")
     dma(A("XO"), T.tx[:, :], "y")
+    iota(A("IOF", 0, 256), [[1, 256]], B0, 0)
+    iota(col("PI", 0), [[1, 1]], 0, 1)
     iota(A("IQ"), [[1, WF]], 0, 0)
-    iota(col("PI", 0), [[1, 1]], 0, 1, False)
-    iota(A("IM"), [[1, 8], [0, 16]], 0, 0)
-    iota(A("IOF", 0, FN // 2), [[1, FN // 2]], B0, 0)
-    for i in range(16):
-        sv = A("SV", i, V, 16)
-        act((sv[0], sv[1], 0, V, i), A("IQ", 0, W), bias=float(W * i + B0), per=1.0 / 16)
-    fill(A("WL"), 0.0)
+    for a, b in ((256, 512), (512, 1024), (1024, 2048), (2048, 3072), (3072, 4096)):
+        act(A("IOF", a, b), A("IOF", 0, b - a), bias=float(a))
+    for a in range(2):
+        iota(A("SV", 1024 * a, 1024 * a + 1024), [[1, 64], [WS, 16]], BI + 64 * a, 0)
+    fill(A("WL"), B0 / 2.0)
     fill(A("ZT"), 0.0)
+    fill(A("CCP", 2 * WS, 4 * WS), 0.0)
     ts(col("PI", 1), col("PI", 0), 15, Op.bitwise_and)
     ts(col("PI", 2), col("PI", 0), 4, Op.arith_shift_right)
     ts(col("PI", 3), col("PI", 0), 15, Op.bitwise_and, 1, Op.arith_shift_right)
     cp(A("CF", 0, 4), A("PI", 0, 4))
+    diag(I1, 1.0)
+    for b in ("CIW", "WA", "WB"):
+        dma(ROW(b, 0, 0, VS), A("ZT", 0, WS))
 
-    ts(A("IC"), A("CCI"), 15, Op.bitwise_and)
-    ts(A("ID"), A("CCI"), 4, Op.arith_shift_right)
-    ts(A("CCP", 2 * W, 3 * W), A("IC"), float(W), Op.mult)
-    cp(A("CCP", 3 * W, 4 * W), A("ID"))
-    dma(ROW("WL", 4, 0, V), A("CCP", 2 * W, 3 * W), "y")
-    dma(ROW("WL", 5, 0, V), A("CCP", 3 * W, 4 * W), "y")
-    tt(A("FE"), A("CCP", 2 * W, 3 * W), A("CCP", 3 * W, 4 * W), Op.add)
-    ts(A("FG"), A("NMI"), float(B0), Op.add)
-    cp(A("CCU"), A("FE"))
-    act(A("CCP", 0, W), A("CCP", 3 * W, 4 * W), scale=16.0)
-    act(A("CCP", W, 2 * W), A("CCP", 2 * W, 3 * W), scale=1.0 / W)
-    def scatter(q, win, off, lo, hi, vals, step=32):
-        for a in range(lo, hi, step):
-            b = min(hi, a + step)
-            if q == "v":
-                cp(IND(A(win), A(off, a, b)), A(vals, 16 * a, 16 * b))
-            else:
-                act(IND(A(win), A(off, a, b)), A(vals, 16 * a, 16 * b), Act.Silu)
-
-    scatter("s", "CIW", "CCU", 0, W, "SV", 64)
-    hilo(A("NH"), A("NL"), A("FG"))
-    dma(ROW("WL", 0, 0, V), A("NH"), "y")
-    dma(ROW("WL", 1, 0, V), A("NL"), "y")
-    for b in ("WA", "WB"):
-        dma(ROW(b, 0, 0, V), A("ZT", 0, W), "y")
+    ts(A("IC", 0, W), A("CCI"), 15, Op.bitwise_and)
+    ts(A("ID", 0, W), A("CCI"), 4, Op.arith_shift_right)
+    sh, sl = A("CCP", 2 * WS, 2 * WS + W), A("CCP", 3 * WS, 3 * WS + W)
+    ts(sh, A("IC", 0, W), float(WS), Op.mult)
+    cp(sl, A("ID", 0, W))
+    rows("WL", 4, "CCP", 2 * WS)
+    mm(A("K0", 0, W), [(I1, sh), (I1, sl)])
+    cp(A("CCU"), A("K0", 0, W))
+    act(A("CCP", 0, W), sl, scale=16.0)
+    act(A("CCP", WS, WS + W), sh, scale=1.0 / WS)
+    act(A("CCP", W, WS), A("IQ", W, WS), scale=16.0)
+    act(A("CCP", WS + W, 2 * WS), A("ZT", 0, 16), bias=cf(PM))
+    cp(A("NH"), A("NMI"))
+    tt(A("NL"), A("NMI"), A("NH"), Op.subtract)
+    dma(ROW("WL", 0, 0, V), A("NH"))
+    dma(ROW("WL", 1, 0, V), A("NL"))
     hand(A("XO", V // 2, V), "hb")
     send(A("XO", 0, V // 2), A("X1", 0, V // 2), "ax0", -1)
     hand(A("CCP"), "hc")
     hand(A("XO", 0, V // 2), "ha")
-    iota(A("FD", 0, L1V), [[16, L1V]], V, 1)
-    iota(A("FD", L1V, WF), [[16, WF - L1V]], V, 1)
-    iota(A("IOF", FN // 2, FN), [[1, FN // 2]], B0 + FN // 2, 0)
-    sigma(A("FA"), A("PLI"), A("IA"), A("FB"), A("FC"), W)
-    ts(col("CF", ZC), col("CF", PG), 16.0, Op.mult, 15.0, Op.add)
-    ts(A("CF", RM, RM + 8), A("IQ", 0, 8), col("CF", PH), Op.is_equal)
+    iota(A("SV", 2048, V), [[1, 64], [WS, 16]], BI + 128, 0)
+    iota(A("FD"), [[0, WF // 64], [16, 64]], VS, 1)
+    iota(A("IM"), [[1, 8], [0, 16]], 0, 0)
+    scatter("s", A("CIW"), "CCU", 0, W, "SV", 32)
+    ts(A("IA"), A("PLI"), 4, Op.arith_shift_right)
+    ts(A("K1", 0, WF), A("PLI"), float(WS), Op.mult)
+    ts(A("FC"), A("IA"), float(1 - VS), Op.mult)
+    tt(A("FA"), A("K1", 0, WF), A("FC"), Op.add)
     cp(A("PLU"), A("FA"))
+    ts(cf(ZC), cf(PG), 16.0, Op.mult, 15.0, Op.add)
+    ts(A("CF", RM, RM + 8), A("IQ", 0, 8), cf(PH), Op.is_equal)
+    ts(cf(R4), cf(PM), 4.0, Op.is_lt)
+    zmat(Z45, cf(RM + 2))
+    zmat(ZN0, cf(R4))
+    ts(A("INV"), A("PLI"), 0.0, Op.is_lt, DEAD, Op.mult)
+    fill(A("MS"), 0.0)
     dma(A("F", B0, B0 + FN), T.fo[:, :], "y", A("PLU"))
-    dma(A("F", 0, B0), T.fo[:, 0:B0], "y", A("PLU"))
-    dma(A("PW1", 0, B0), T.fo[:, 0:B0], "y", A("PLU"))
+    dma(A("PW", 0, B0), T.fo[:, 0:B0], "y", A("PLU"))
+    fill(A("F", 0, B0), 1024.0)
+    ext(A("PV", 0, W), "WL", 0, V, ZN0)
+    pass_names(0, A("PV", 0, W))
     for h in range(4):
         lo, hi = h * WF // 4, (h + 1) * WF // 4
-        ts(A("PW1", B0 + 16 * lo, B0 + 16 * hi), IND(A("WL"), A("PLU", lo, hi)), rm(2), Op.mult)
-        if h == 0:
-            ts(A("Z"), A("IQ", 0, 144), col("CF", ZC), Op.is_equal)
-            ts(A("I1"), A("IQ", 0, 128), col("CF", PF), Op.is_equal)
-            ts(A("INV"), A("PLI"), 0.0, Op.is_lt, 8192.0, Op.mult)
-            ts(A("ZR"), A("IQ", 0, 144), col("CF", ZC), Op.is_equal, col("CF", RM), Op.mult)
-        ext(A("PC" if h < 3 else "PA", lo, hi), "PW1", B0 + 16 * lo, B0 + 16 * hi, more=[(A("I1"), A("INV", lo, hi))])
-        if h == 1:
-            ext(A("PV", 0, W), "WL", 0, V, "ZR")
-    tt(A("FA", 0, W), A("PC", 0, W), A("FD", 0, W), Op.min)
-    cp(A("N0U"), A("PV", 0, W))
-    send(A("N0U"), A("N1"), "an1", -1)
-    tt(A("FA", W, WF), A("PA", W, WF), A("FD", W, WF), Op.min)
-    cp(A("YU"), A("FA"))
-    dma(A("TC"), ROW("CIW", 0, 0, V), "y")
-    act(IND(A("WB"), A("YU", L1V, WF)), A("IOF", 16 * L1V, FN), Act.Silu)
-    cp(IND(A("WA"), A("YU", 0, L1V)), A("IOF", 0, 16 * L1V))
-    dma(A("TA", 0, W), ROW("WA", 0, 0, V), "y")
-    dma(A("TB", 0, W), ROW("WB", 0, 0, V), "s")
-    ts(A("CIU"), A("TC"), B0 - 0.25, Op.subtract)
+        bank = A("J%d" % (h % 3), lo, hi)
+        gather("v" if lo < YV else "s", A("PW", B0 + 16 * lo, B0 + 16 * hi), A("WL"), A("PLU", lo, hi))
+        mm(bank, [(I1, A("INV", lo, hi))], last=False)
+        ext(bank, "PW", B0 + 16 * lo, B0 + 16 * hi, Z45, first=False)
+        tt(A("FA", lo, hi), bank, A("FD", lo, hi), Op.min)
+        cp(A("YU", lo, hi), A("FA", lo, hi))
+    scatter("v", A("WA"), "YU", 0, L1V, "IOF", 48)
+    scatter("s", A("WB"), "YU", L1V, WF, "IOF", 56)
+    dma(A("TA", 0, WS), ROW("WA", 0, 0, VS), "y")
+    dma(A("TB", 0, WS), ROW("WB", 0, 0, VS), "s")
+    dma(A("TC"), ROW("CIW", 0, 0, VS), "s")
+    ts(A("CIU"), A("TC", 0, W), float(BI), Op.subtract)
     for t in (1, 2, 3):
         send(A("CIU"), A("CI%d" % t), "ai%d" % t, -t)
-    ts(A("I2"), A("IQ", 0, 128), col("CF", PF), Op.is_equal, 2.0, Op.mult)
-    ts(A("IN2"), A("IQ", 0, 128), col("CF", PF), Op.is_equal, -2.0, Op.mult)
-    ts(A("IN1"), A("IQ", 0, 128), col("CF", PF), Op.is_equal, -1.0, Op.mult)
-    ts(A("IDF"), A("IQ", 0, 128), col("CF", PF), Op.is_equal)
-    ts(A("BO"), A("IM"), col("CF", PG), Op.is_equal)
-    run("g", lambda: g.affine_select(T.TRI[:, :], T.BO[:, :], [[1, 128]], Op.is_ge, 0.0, 0, -1), A("TRI"), [A("BO")])
-    fill(A("ZB"), 0.0)
-    fill(A("RC", 0, 1), 0.0)
-    fill(A("YT"), 0.0)
-    ts(col("CF", PW_), col("CF", PM), float(W), Op.mult)
-
-    def fn_gather(t, c):
-        act(A("FNB", c * CH, (c + 1) * CH), IND(A("F"), A("N%d" % t, c * CH // 16, (c + 1) * CH // 16)))
-
-    for c in range(NCH):
-        fn_gather(1, c)
-    cp(A("NF"), A("N1"))
-    tt(A("FE"), A("TA", 0, W), A("TB", 0, W), Op.add)
-    ts(A("LU"), A("FE"), 0.25, Op.add)
-    dma(A("WA", 0, FN), A("IOF"), "y", A("LU"))
-    for b in ("WA", "WB"):
-        dma(ROW(b, 0, 0, FN), A("ZT"), "y")
-    dma(A("WN"), T.tx[:, :], "y", A("YU"))
-    dma(A("PW2", 0, FN), T.fo[:, :], "y", A("LU"))
-    dma(A("PW2", FN, FN + B0), T.fo[:, 0:B0], "y", A("LU"))
+    ts(A("IC"), A("TC"), float(BI), Op.subtract, 0.0, Op.max)
+    cp(A("CIH", 0, WS), A("IC"))
+    tt(A("CIH", WS, 2 * WS), A("IC"), A("CIH", 0, WS), Op.subtract)
+    send(A("CIH"), A("CH1"), "ah", -1)
 
     def kt(j):
         return A("KT", 16 * j, 16 * j + K)
 
     def ku(j):
         return A("KU", 16 * j, 16 * j + K)
-    KW, KH, DTR, DPW, VAL, DFI, T1V, NW, NM_, DM, T1, T2, K1, K2, K3, K4, K5 = [kt(j) for j in range(17)]
-    A16, CWB = A("KH2", 0, K), A("KH2", 16, 16 + K)
+    KW, KF, K1_, K2_, K3_, K4_ = [kt(j) for j in range(6)]
+    diag(I2, 2.0)
+    diag(IN2, -2.0)
+    diag(IN1, -1.0)
+    diag(IDF, 1.0)
+    diag(I256, 256.0)
+    diag(INB, -OUT)
+    zmat(ZALL)
+    zmat(Z16, 16.0)
+    zmat(ZWS, float(WS))
+    zmat(Z01, cf(RM))
+    ts(cf(RD), cf(PM), 2.0, Op.is_equal, -DEAD, Op.mult)
+    ts(cf(RL), cf(RD), cf(RM), Op.add)
+    zmat(ZL, cf(RL))
+    zmat(Z67, cf(RM + 3))
+    zmat(Z89, cf(RM + 4))
+    zmat(ZAB, cf(RM + 5))
+    ts(BO, A("IM"), cf(PG), Op.is_equal)
+    ts(BO45, A("IM"), cf(PG), Op.is_equal, cf(RM + 2), Op.mult)
+    pick(TRI, BO, [[1, 128]], 0)
+    for i in range(1, 16):
+        pick(TDm(i), BO, [[16, 8], [0, 16]], i - 1)
+    fill(A("ZB"), 0.0)
+    fill(A("RC", 0, 1), 0.0)
+    fill(A("FREE", W, WS), 1.0)
+    fill(A("LHL"), 0.0)
+    fill(A("CB"), -float(K))
+    fill(A("YT"), 0.0)
+    ts(cf(PW_), cf(PM), float(WS), Op.mult)
+    ts(cf(R12), cf(PM), float(K), Op.is_lt)
+    ts(KW, A("IQ", 0, K), 16.0, Op.mult, cf(PM), Op.add)
+    ts(KF, KW, OUT - FB, Op.add)
+    iota(A("DMP"), [[0, K], [16, 16]], 16 - FB, 1)
+    act(A("IDT", 0, WS), A("ZB"), bias=cf(PW_))
+    act(A("IDT", WS, 2 * WS), A("IQ", 0, WS))
+    act(A("IDT", 2 * WS, 3 * WS), A("IQ", 0, WS), scale=16.0, bias=float(B0))
+    act(A("IDT", 3 * WS, 4 * WS), A("ZB"), bias=cf(PM))
+    dma(A("WN", 0, V), T.tx[:, :], "y", A("YU"))
+    dma(A("WN", V, VS), T.tx[:, 0:VS - V], "y", A("YU"))
+    dma(ROW("WN", 2, 0, VS), A("ZB"))
 
-    def late_constants(c):
-        if c == 0:
-            act(A("KB"), A("IQ", 0, W))
-            act(A("IDT", W, 2 * W), A("IQ", 0, W))
-            act(A("IDT", 0, W), A("ZB"), bias=col("CF", PW_))
-            act(A("IDT", 2 * W, 3 * W), A("IQ", 0, W), scale=16.0)
-            act(A("IDT", 3 * W, 4 * W), A("ZB"), bias=col("CF", PM))
-            for r in range(4):
-                dma(ROW("WN", r, 0, V), A("IDT", r * W, (r + 1) * W), "y")
-            for r in range(2):
-                dma(ROW("PW2", r, 0, V), A("ZB"), "y")
-                dma(ROW("PW2", r, V, FN + B0), A("ZB", 0, (FN + B0 - V) // 16), "y")
-            ts(KW, A("IQ", 0, K), 16.0, Op.mult, col("CF", PM), Op.add)
-            ts(col("CF", R12), col("CF", PM), float(K - 1), Op.is_lt)
-            ts(col("CF", LO1), col("CF", PM), 1.0, Op.is_equal)
-            ts(col("CF", R0), col("CF", PM), 0.0, Op.is_equal)
-        if c == 1:
-            ts(A("BO256"), A("IM"), col("CF", PG), Op.is_equal, 256.0, Op.mult)
-            ts(A("Z192"), A("IQ", 0, 144), col("CF", ZC), Op.is_equal, float(W), Op.mult)
-            for t in range(1, TV + 1):
-                ts(col("ZM", t), col("CF", PM), float((STEP * t) % V % 16), Op.is_lt)
-        if c == 2:
-            act(KH, KW, bias=-0.5, scale=0.5)
-            act(DTR, KW, bias=float(V))
-            act(DPW, KW, bias=float(B0 + FN))
-            act(DFI, KW, bias=float(FN + V - 16 * FINS))
+    tt(A("ID"), A("TA", 0, WS), A("TB", 0, WS), Op.add)
+    cp(A("LU"), A("ID", 0, W))
+    cp(LH, A("ID", 0, W))
+    tt(LL, A("ID", 0, W), LH, Op.subtract)
+    dma(A("WA", FB, FB + FN), A("IOF"), "y", A("LU"))
+    for b in ("WA", "WB"):
+        dma(ROW(b, 0, FB, FB + FN), A("ZT"))
 
-    LQ = 64
+    def rg(c):
+        return c * CH, (c + 1) * CH
 
-    def pre_ops(t, c):
-        if c == 0:
-            if t == 1:
-                cp(A("LF"), A("LU"))
-            else:
-                cp(A("LU", LQ, W), A("PA", 0, W - LQ))
-                act(A("LF", 0, LQ), A("PC", 0, LQ))
-                act(A("LF", LQ, W), A("PA", 0, W - LQ))
-            act(A("NH"), A("NF"))
-            act(A("LH"), A("LF"))
-            mm(A("PA", 0, W), [(A("IDF"), A("NF")), (A("IN1"), A("NH"))])
-            mm(A("PC", W, 2 * W), [(A("IDF"), A("LF")), (A("IN1"), A("LH"))])
-            mm(A("PC", 0, W), [(A("I1"), A("LH"))])
-            act(A("RR"), A("LH"), Act.Relu, bias=float(B0), scale=-1.0)
-            act(A("NL"), A("PA", 0, W))
-            act(A("LL"), A("PC", W, 2 * W))
-        if c == 1:
-            mm(A("PK", 0, W), [(A("I1"), A("LH")), (A("I1"), A("LL")), (A("IN1"), A("NH")), (A("IN1"), A("NL"))])
-            dma(ROW("WN", 4, 0, V), A("NH"), "y")
-            dma(ROW("WN", 5, 0, V), A("NL"), "y")
-            if t < TV:
-                for r in range(4 if t < 3 else 2):
-                    dma(ROW("WN", 2 + 4 * t + r, 0, V), A("CC%d" % t, r * W, (r + 1) * W), "y")
-            act(A("AB"), A("PK", 0, W), Act.Abs)
-            act(A("E1"), A("AB"), Act.Relu, bias=100.0, scale=-100.0)
-        if c == 2 and t == TV:
-            ts(A("IC"), A("LF"), float(B0), Op.subtract)
-            act(A("DMP", 0, FINS), A("IQ", 0, FINS), bias=col("CF", PM), scale=16.0)
-            act(A("DMP", FINS, W), A("IQ", 0, W - FINS), bias=col("CF", PM), scale=16.0)
-            act(A("DMP"), A("DMP"), bias=float(FN))
-            act(A("FG"), A("LF"), bias=float(-B0 * WF), scale=float(WF))
-            ts(A("ID"), A("IC"), 4, Op.arith_shift_right)
-            act(A("FH"), A("DMP"), scale=-1.0)
-        if c == 3 and t == TV:
-            ts(A("FE"), A("ID"), float(1 - FN), Op.mult)
-            mm(A("PB", 0, W), [(A("IDF"), A("FE")), (A("IDF"), A("FG")), (A("IDF"), A("FH"))])
-            act(A("SD"), A("PB", 0, W))
+    def named(t):
+        x = "X%d" % t
+        for c in range(NCH):
+            lo, hi = rg(c)
+            off = A("NR", W * (t - 1) + lo // 16, W * (t - 1) + hi // 16)
+            gather("v" if lo >= V - FNV else "s", A("FNB", lo, hi), A("F"), off)
+            if KIND[c] == "E":
+                mm(A("PV"), [(I1, A(x, lo, hi)), (IN1, A("FNB", lo, hi))])
+                act(A("AQ", lo, hi), A("PV"), Act.Abs)
+
+    def tables(t):
+        rows("WL", 0, "LHL", 0)
+        rows("WN", 0, "MR", 2 * WS * (t - 1))
+        if t == 1:
+            rows("WN", 4, "IDT", 0)
+            rows("WN", 8, "CC1", 2 * WS)
+        if t == 2:
+            rows("WN", 4, "CH1", 0)
+            rows("WN", 10, "CC2", 2 * WS)
+        if t == TV:
+            rows("WN", 4, "IDT", 2 * WS)
+        else:
+            rows("WN", 6, "CC%d" % t, 0)
 
     def judge(t):
         x = "X%d" % t
-        sb = ["S0", "S1", "S2"]
-
-        def rg(c):
-            return c * CH, (c + 1) * CH
-
-        def listed(c):
-            return IND(A("F"), A("LU", c * CH // 16, (c + 1) * CH // 16))
-
-        bank = {0: "S0", 1: "S1", 2: "S2", 3: "PA", 4: "S1", 5: "S0"}
-
-        def u(c):
+        mm(A("PL", 0, W), [(I1, halves("MR", t - 1, 0)), (I1, halves("MR", t - 1, 1)), (IN1, LH), (IN1, LL)])
+        ts(A("THR"), A("PL", 0, W), 0.0, Op.is_equal, 100.0, Op.mult)
+        tables(t)
+        if t == TV:
+            mm(A("PD", 0, W), [(I1, LH), (I1, LL)])
+            ts(A("IC", 0, W), A("PD", 0, W), 1.0 / 16, Op.mult, -0.47, Op.add)
+            ts(A("FE"), A("IC", 0, W), float(1 - FN), Op.mult)
+            mm(A("PD", 0, W), [(I256, LH), (I256, LL), (IDF, A("FE"))], last=False)
+        na, ne = 0, 0
+        for c in range(NCH):
             r = rg(c)
-            mm(A(bank[c]), [(A("IN2"), A(x, *r)), (A("I2"), A("FNB", *r))], last=False)
-            tt(A("U", *r), listed(c), A("FNB", *r), Op.subtract)
-            mm(A(bank[c]), [(A("I1"), A("U", *r))], first=False)
-
-        def u_scalar(c):
-            r = rg(c)
-            mm(A("PB"), [(A("I1"), A("U", *r)), (A("IN1"), A("FNB", *r))])
-            mm(A(bank[c]), [(A("IN2"), A(x, *r)), (A("I1"), A("FNB", *r)), (A("I1"), A("U", *r))])
-            act(A("U", *r), A("PB"), Act.Sign)
-
-        def prod(c, own=False):
-            r = rg(c)
-            tt(A("U", *r), A(bank[c]), A("U", *r), Op.mult)
-            if own:
-                ts(A("U", *r), A("U", *r), 0.0, Op.is_ge, 0.5, Op.subtract)
+            u = A("U", *r)
+            listed = A("LU", r[0] // 16, r[1] // 16)
+            if KIND[c] == "E":
+                bank = A("K%d" % (ne % 2))
+                ne += 1
+                gather("s", u, A("F"), listed)
+                mm(bank, [(I1, A(x, *r)), (IN1, u)])
+                act(u, bank, Act.Abs)
+                mm(bank, [(I1, u), (IN1, A("AQ", *r))])
+                act(u, bank, Act.Sign, bias=0.5)
             else:
-                act(A("U", *r), A("U", *r), Act.Sign, bias=0.5)
-
-        def votes(c0, c1):
-            lo, hi = c0 * CH, c1 * CH
-            a, b = lo // 16, hi // 16
-            mm(A("PV", a, b), [(A("IN1"), A("E1", a, b)), (A("I1"), A("RR", a, b))], last=False)
-            mm(A("PV", a, b), [(A("Z", 15 - i, 143 - i), A("U", lo + i, hi, 16)) for i in range(16)], first=False)
-
-        def more(c):
-            pre_ops(t, c)
-            if t == 1:
-                late_constants(c)
-
-        u(0)
-        more(0)
-        u(1)
-        act(A("U", *rg(3)), listed(3))
-        prod(0)
-        u(2)
-        u_scalar(3)
-        more(1)
-        act(A("U", *rg(4)), listed(4))
-        prod(1)
-        u(5)
-        u_scalar(4)
-        more(2)
-        prod(2)
-        votes(0, 2)
-        more(3)
-        prod(3, True)
-        votes(2, 4)
-        prod(5, True)
-        prod(4, True)
-        votes(4, 6)
-
-    def look(buf, win, off, pair, out):
-        ts(A(buf), IND(win, off), rm(pair), Op.mult)
-        ext(out, buf, 0, W)
+                bank = A("J%d" % (na % 3))
+                na += 1
+                mm(bank, [(IN2, A(x, *r)), (I2, A("FNB", *r))], last=False)
+                tt(u, IND(A("F"), listed), A("FNB", *r), Op.subtract)
+                mm(bank, [(I1, u)], first=False)
+                tt(u, bank, u, Op.mult)
+                if KIND[c] == "A":
+                    ts(u, u, 0.0, Op.is_ge, 0.5, Op.subtract)
+                else:
+                    act(u, u, Act.Sign, bias=0.5)
+            if c % 2:
+                ext(A("PV", (c - 1) * CH // 16, (c + 1) * CH // 16), "U", (c - 1) * CH, (c + 1) * CH)
 
     def recount(t):
         s = (STEP * t) % V
         sc = s // 16
         last = t == TV
-        pa, pb = A("PA", 0, K), A("PB", 0, K)
-        ts(A("FREE"), A("PV", 0, W), 0.0, Op.is_ge)
-        act(A("ALV"), A("FREE"), bias=1.0, scale=-1.0)
-        run("v", lambda: g.vector.tensor_tensor_scan(T.RC[:, 1:W + 1], T.FREE[:, :], T.ZB[:, :], 0.0, Op.add, Op.add),
-            A("RC", 1, W + 1), [A("FREE"), A("ZB")])
-        ts(col("RC", W + 1), col("FREE", sc), col("ZM", t), Op.mult, col("RC", sc), Op.add)
-        mm(A("S2", 0, 2), [(A("BO"), A("RC", W, W + 2))])
-        mm(A("S1", 0, 1), [(A("Z", 15 - i, 143 - i), col("RC", 16 * i + 16)) for i in range(K)])
-        mm(pb, [(A("Z", 15 - i, 143 - i), A("RC", i + 1, W + 1, 16)) for i in range(16)])
-        mm(A("S0", 0, W), [(A("BO"), A("RC", 0, W)), (A("TRI"), A("FREE"))])
+        g1 = A("G1", W * (t % 2), W * (t % 2) + W)
+        g1r = (g1[2], g1[3])
+        free = A("FREE", 0, W)
+        tt(free, A("PV", 0, W), A("THR"), Op.is_ge)
         if not last:
-            tt(A("DH"), A("PC", 0, W), A("ALV"), Op.mult)
-            tt(A("DL"), A("PC", W, 2 * W), A("ALV"), Op.mult)
-            dma(ROW("WL", 4, 0, V), A("DH"), "y")
-            dma(ROW("WL", 5, 0, V), A("DL"), "y")
-        else:
-            tt(A("PV", 0, W), A("ALV"), A("SD"), Op.mult)
-            tt(A("FG"), A("PV", 0, W), A("DMP"), Op.add)
-            cp(A("FOU"), A("FG"))
-        act(A("BW", 0, K), pb)
-        act(A("CUM"), A("S0", 0, W))
+            rows("WL", 2, "FREE", 0, 1)
+        run("v", lambda: g.vector.tensor_tensor_scan(T.RC[:, 1:WS + 1], T.FREE[:, :], T.ZB[:, :], 0.0, Op.add, Op.add),
+            A("RC", 1, WS + 1), [A("FREE"), A("ZB")])
+        tot, cs = col("PV", 200), col("PV", 201)
+        mm(tot, [(BO, col("RC", W)), (BO, col("CB", 0))])
+        mm(cs, [(BO, col("RC", sc)), (TDm(s % 16), col("FREE", sc))])
+        mm(col("K0", 16), [(zs(ZALL, i), col("RC", 16 * i + 16)) for i in range(K)])
+        ext(A("J0", 0, K + 1), "RC", 1, WS + 1)
+        mm(A("J0", 16, 16 + WS), [(BO, A("RC", 0, WS)), (TRI, A("FREE"))])
+        act(A("BW", 0, K + 1), A("J0", 0, K + 1))
+        act(A("CUM"), A("J0", 16, 16 + WS))
+        mm(A("J2", 0, W), [(I1, A("ZB", 0, W))], last=False)
         if last:
-            scatter("s", "WB", "FOU", 0, FINS, "IOF", 16)
-            scatter("v", "WA", "FOU", FINS, W, "IOF", 8)
+            mm(A("PD", 0, W), [(INB, free)], first=False)
+            tt(A("FG"), A("PD", 0, W), A("DMP"), Op.max)
+            ts(A("FOU"), A("FG"), float(FB - 16), Op.add)
+            scatter("s", A("WB"), "FOU", 0, FINS, "IOF", 16)
+            scatter("v", A("WA"), "FOU", FINS, W, "IOF", 8)
         else:
             for lo in range(0, V - TRV, CH):
                 hi = min(lo + CH, V - TRV)
-                act(A("TR", lo, hi), IND(A("WL"), A("CI%d" % t, lo // 16, hi // 16)), scale=rm(2))
+                gather("s", A("TR", lo, hi), A("WL"), A("CI%d" % t, lo // 16, hi // 16))
             for lo in range(V - TRV, V, 256):
-                ts(A("TR", lo, lo + 256), IND(A("WL"), A("CI%d" % t, lo // 16, lo // 16 + 16)), rm(2), Op.mult)
-        tot, cs = col("S2", 0), col("S2", 1)
+                gather("v", A("TR", lo, lo + 256), A("WL"), A("CI%d" % t, lo // 16, lo // 16 + 16))
         base = A("PV", 256, 256 + W)
-        ts(col("SC", 0), tot, float(C), Op.subtract, cs, Op.min)
-        ts(col("SC", 1), col("SC", 0), 0.0, Op.max)
-        ts(col("SC", 2), col("SC", 1), -1.0, Op.mult, cs, Op.add)
-        ts(base, A("IQ", 0, W), col("SC", 2), Op.is_ge, col("SC", 1), Op.mult)
+        ts(col("SC", 0), tot, 0.0, Op.max, cs, Op.min)
+        ts(col("SC", 1), col("SC", 0), -1.0, Op.mult, cs, Op.add)
+        ts(base, A("IQ", 0, W), col("SC", 1), Op.is_ge, col("SC", 0), Op.mult)
         tt(A("TAU"), base, A("IQ", 0, W), Op.add)
-        ts(A("CMA"), A("TAU"), col("S1", 0), Op.is_ge, col("CF", R12), Op.mult)
+        ts(A("CMA"), A("TAU"), col("K0", 16), Op.is_ge, cf(R12), Op.mult)
+        pa, pb, pc = A("K0", 0, K), A("K1", 0, K), A("J1", 0, K)
         ext(pa, "CMA", 0, W)
-        ts(VAL, KW, tot, Op.is_lt)
-        tt(A("AD"), A("PK", 0, W), A("ALV"), Op.mult)
-        mm(A("S2", 0, W), [(A("I1"), A("NH")), (A("I1"), A("NL")), (A("IDF"), A("AD"))])
-        cp(ku(0), pa)
-        tt(A("CMB"), IND(A("BW", 0, K), ku(0)), A("TAU"), Op.is_le)
-        ts(A16, pa, 16.0, Op.mult)
-        ext(pb, "CMB", 0, W, more=[(A("I1"), A16)])
+        ext(pb, "CMA", 0, W, Z16, last=False)
+        ext(pc, "CMA", 0, W, Z16, last=False)
+        nb = A("J0" if last else "PD", 0, W)
+        tt(A("FP"), A("PL", 0, W), free, Op.mult)
+        mm(nb, [(I1, LH), (I1, LL), (IDF, A("FP"))])
         if not last:
-            cp(A("NS%d" % t), A("S2", 0, W))
-            send(A("NS%d" % t), A("N%d" % (t + 1)), "an%d" % (t + 1), -1)
+            pass_names(t, nb)
         else:
-            ts(A("FH"), A("S2", 0, W), float(B0), Op.subtract)
-        ts(ku(1), pb, float(W - 1), Op.min)
+            ts(A("FH"), nb, float(B0), Op.subtract)
+        cp(ku(0), pa)
+        tt(A("CMB"), IND(A("BW", 0, K + 1), ku(0)), A("TAU"), Op.is_le)
+        ext(pb, "CMB", 0, W, first=False)
+        ext(pc, "CMB", 0, W, first=False, last=False)
+        cp(ku(1), pb)
         tt(A("CMC"), IND(A("CUM"), ku(1)), A("TAU"), Op.is_le)
-        cp(CWB, pb)
-        ext(pa, "CMC", 0, W, "Z192", more=[(A("I1"), CWB)])
-        if t in (2, 3):
-            cp(IND(A("PW%d" % (t - 1)), ku(5)), A("GI"))
+        ext(pc, "CMC", 0, W, ZWS, first=False)
+        cp(ku(2), pc)
+        cp(g1, IND(A("WN"), ku(2)))
+        ext(pa, "G1", g1r[0], g1r[1], Z01)
+        mm(A("K1", 0, W), [(TDm(2), g1)])
+        for j in range(K):
+            ts(A("EB", W * j + 16 * j, W * j + W), A("K1", 16 * j, W), col("K0", j), Op.is_equal, -4.0, Op.mult)
+            if j < K - 1:
+                mm(A("J2", 16 * j + 16, W), [(BO, A("EB", W * j + 16 * j + 16, W * j + W))], False, False)
+        mm(A("J2", 0, W), [(TDm(i), A("EB", i, WS * (K - 1) + i + 1, WS), A("J2", i, W, 16)) for i in range(1, 16)],
+           False, False)
         if last:
             for gi in range(8):
                 for h in range(2):
-                    mm(A("S0", 32 * gi + 16 * h, 32 * gi + 16 * h + 16, parts=W // 2),
+                    mm(A("J0", 32 * gi + 16 * h, 32 * gi + 16 * h + 16, parts=W // 2),
                        [(A("FH", h, W, 2), A("IDF", 16 * gi, 16 * gi + 16))])
-        ts(ku(2), pa, float(V - 1), Op.min)
-        ts(A("GN"), IND(A("WN"), ku(2)), rm(2), Op.mult)
-        ext(pb, "GN", 0, W)
-        mm(A("PK", 0, W), [(A("BO256"), A("GN")), (A("I1"), A("KB"))])
-        if not last:
-            look("GC", A("WN"), ku(2), 1 + 2 * t, pa)
-            cp(ku(3), pb)
-        else:
-            ts(A("GC"), IND(A("WN"), ku(2)), rm(1), Op.mult)
-            mm(A("PC", 0, W), [(A("BO"), A("GC"))])
-        ts(K2, pb, -256.0, Op.mult)
-        cp(NW, pb)
-        tt(NM_, K2, KH, Op.subtract)
-        if not last:
-            cp(A("GP"), IND(A("PW1", 0, B0 + FN), ku(3)))
-            ext(pb, "GP", 0, W)
-        seg = []
-        o = 0
-        for j in range(K):
-            w = 16 * (j + 1)
-            seg.append(A("DD", o, o + w))
-            o += w
-            act(seg[j], A("PK", 0, w), bias=col("KT", 16 * 8 + j))
-        red = [0]
-
-        def reduce(m):
-            for j in range(red[0], min(K, red[0] + m)):
-                out = col("KT", 16 * 9 + j)
-                run("v", lambda j=j, out=out: g.vector.tensor_reduce(out[1], seg[j][1], AxisListType.X, Op.min,
-                                                                     apply_absolute_value=True), out, [seg[j]])
-            red[0] = min(K, red[0] + m)
-
-        if last:
-            dma(A("TB"), ROW("WB", 0, 0, FN), "s")
-            cp(A("YT", 0, WF, parts=W // 2), A("S0", 0, WF, parts=W // 2))
+            dma(A("TB"), ROW("WB", 0, FB, FB + FN), "s")
+            act(A("YT", 0, WF, parts=W // 2), A("J0", 0, WF, parts=W // 2))
             send(A("YT"), A("YL"), "ay", TV)
-            ts(A("KI", 0, K), NW, float(B0), Op.subtract)
-            ts(A("FV"), A("PC", 0, W), float(B0), Op.add)
-            sigma(K3, A("KI", 0, K), A("KI", 16, 16 + K), K1, K2, WF)
-            reduce(4)
-            tt(T1, K3, DFI, Op.subtract)
-            reduce(4)
-            cp(ku(3), K3)
-            ts(A("GP"), IND(A("WA", 0, FN), ku(3)), 1.0, Op.is_lt, col("CF", R0), Op.mult)
-            ext(pb, "GP", 0, W)
-            tt(T2, T1, VAL, Op.mult)
-            tt(T1V, pb, T2, Op.mult)
-            reduce(K)
-            tt(K1, DM, KH, Op.is_gt)
-            tt(K2, T1V, K1, Op.mult)
-            tt(K4, K2, DFI, Op.add)
-            cp(ku(4), K4)
+            mm(A("PV", 0, W), [(BO45, g1)])
+            cp(A("FV"), A("PV", 0, W))
+            ts(A("KI", 0, K), pa, 1.0 / 16, Op.mult, -0.47, Op.add)
+            ts(K1_, pa, float(WF), Op.mult, -16.0, Op.add)
+            ts(K2_, A("KI", 0, K), float(FN - 1), Op.mult)
+            tt(K3_, K1_, K2_, Op.subtract)
+            cp(ku(3), K3_)
+            mm(pc, [(IDF, K3_)], last=False)
+            ts(A("GL"), IND(A("WA", FB, FB + FN), ku(3)), 1.0, Op.is_lt)
+            mm(A("J2", 0, W), [(TDm(1), A("GL"))], first=False)
+            ts(A("KEEP"), A("J2", 0, W), 0.5, Op.is_ge, OUT / 256, Op.mult)
+            ext(pc, "KEEP", 0, W, Z16, first=False)
+            tt(K4_, pc, KF, Op.max)
+            ts(ku(4), K4_, FB - OUT, Op.add)
             cp(IND(A("WA"), ku(4)), A("FV"))
-            dma(A("TA"), ROW("WA", 0, 0, FN), "y")
-            ts(A("PA", 0, WF), A("TB"), 1.0, Op.is_lt)
-            ts(A("IA"), A("TB"), float(B0), Op.subtract)
-            tt(A("PB", 0, WF), A("PA", 0, WF), A("TA"), Op.mult)
-            tt(A("FC"), A("PB", 0, WF), A("IA"), Op.add)
-            ts(A("YO"), A("FC"), -1.0, Op.max)
+            dma(A("TA"), ROW("WA", 0, FB, FB + FN), "y")
+            act(A("PL", 0, WF), A("TB"), scale=-32.0, bias=-float(B0))
+            ts(A("IA"), A("TB"), float(B0), Op.subtract, -1.0, Op.max)
+            tt(A("PL", WF, 2 * WF), A("PL", 0, WF), A("TA"), Op.add)
+            tt(A("YO"), A("PL", WF, 2 * WF), A("IA"), Op.max)
             for gi in range(8):
                 dma(T.yn[gi, :], A("YL", 32 * gi, 32 * gi + 32, parts=W // 2), "s")
             dma(T.yp[:, :], A("YO"), "y")
             return
-        if t == 1:
-            act(A("GI"), IND(A("WN"), ku(2)), scale=rm(0))
-        if t == 2:
-            act(A("GI"), IND(A("WN"), ku(2)), scale=rm(0), bias=col("CF", LO1))
-        for c in range(NCH):
-            fn_gather(t + 1, c)
-        tt(T1, pa, DTR, Op.subtract)
-        if t == 3:
-            look("GI", A("PW2", 0, B0 + FN), ku(3), 0, pa)
-        reduce(3)
-        cp(ku(4), pb)
+        cp(ku(3), pa)
+        cp(A("GP"), IND(A("PW"), ku(3)))
+        ext(pc, "GP", 0, W, Z45)
+        cp(ku(4), pc)
+        ext(A("J0", 0, K), "G1", g1r[0], g1r[1], Z67)
+        cp(ku(7), A("J0", 0, K))
         pos = ku(4)
-        if t >= 2:
-            look("GP", A("WN"), pos, 4, pb)
-            if t == 3:
-                ts(K1, pa, 0.5, Op.is_lt)
-                ts(K2, pa, 1.0, Op.subtract, 0.0, Op.max)
-                reduce(2)
-                tt(K3, pb, K1, Op.mult)
-                tt(K4, K3, K2, Op.add)
-                cp(ku(5), K4)
-                look("GP", A("WN"), ku(5), 6, pb)
-            reduce(4)
-            cp(ku(6), pb)
-            pos = ku(6)
-        look("GP", A("WL"), pos, 2, pb)
-        tt(T1V, T1, VAL, Op.mult)
-        reduce(3)
-        tt(K2, pb, NW, Op.not_equal)
-        reduce(1)
-        tt(K3, K2, T1V, Op.mult)
-        reduce(K)
-        tt(K1, DM, KH, Op.is_gt)
-        tt(K4, K1, K3, Op.mult)
-        tt(K5, K4, DTR, Op.add)
-        cp(ku(7), K5)
-        cp(IND(A("TR"), ku(7)), A("GN"))
-        ext(A("PC", 0, LQ), "TR", 0, 16 * LQ)
-        ext(A("PA", 0, W - LQ), "TR", 16 * LQ, V)
+        for v in range(1, t):
+            cp(A("GP"), IND(A("WN"), pos))
+            ext(pc, "GP", 0, W, (Z89, ZAB)[v - 1])
+            pos = ku(4 + v)
+            cp(pos, pc)
+        named(t + 1)
+        tt(A("GL"), IND(A("WL"), pos), g1, Op.not_equal)
+        mm(A("J2", 0, W), [(TDm(3), A("GL"))], first=False)
+        ts(A("KEEP"), A("J2", 0, W), 0.5, Op.is_ge)
+        tt(IND(A("TR"), ku(7)), g1, A("KEEP"), Op.mult)
+        ext(A("PL", 0, LQ), "TR", 0, 16 * LQ, ZL)
+        ext(A("PD", 0, W), "TR", 0, V, ZL)
+        cp(A("LU", 0, LQ), A("PL", 0, LQ))
+        cp(A("LU", LQ, W), A("PD", LQ, W))
+        act(LH, A("PD", 0, W))
+        tt(LL, A("PD", 0, W), LH, Op.subtract)
         if t < 3:
-            tt(T2, NW, DPW, Op.subtract)
-            tt(K3, K2, VAL, Op.mult)
-            tt(K4, K1, T2, Op.mult)
-            cp(A("NF"), A("N%d" % (t + 1)))
-            tt(K5, K4, K3, Op.mult)
-            cp(A("LU", 0, LQ), A("PC", 0, LQ))
-            tt(K4, K5, DPW, Op.add)
-            cp(ku(5), K4)
-        else:
-            cp(A("NF"), A("N%d" % (t + 1)))
-            cp(A("LU", 0, LQ), A("PC", 0, LQ))
+            tt(A("KV"), g1, A("KEEP"), Op.mult)
+            ext(A("PD", 0, K), "KV", 0, W, Z01)
+            tt(K4_, A("PD", 0, K), KW, Op.max)
+            cp(ku(8), K4_)
+            cp(IND(A("PW"), ku(8)), g1)
 
+    named(1)
     for t in range(1, TV + 1):
         judge(t)
         recount(t)

from concourse.mybir import AluOpType as Op, AxisListType, ActivationFunctionType as Act

V, FN, C, STEP, TV = 3072, 4096, 192, 745, 4
W = V // 16
WS = W + 16
VS = 16 * WS
WF = FN // 16
K = C // 16
B0 = 256
BI = 64
DEAD = 8192.0
OUT = 16384.0
FB = 512
CH = 512
NCH = V // CH
L1V = 176
YV = 256
FINS = 144
TRV = 512
FNV = 0
KIND = "AEAEAB"
LQ = 64

CYC, PEC, HOP, GATH, SCAT = 0.0009, 0.00045, 0.08, 1.56, 3.8

f32, bf, i32, u16 = "float32", "bfloat16", "int32", "uint16"
SCRATCH = {}


def _sb(names, cols, dtype):
    for n in names.split():
        SCRATCH[n] = ("sbuf", [128, cols], dtype)


_sb("XO X1 X2 X3 X4 FNB U AQ", V, bf)
_sb("WN WL", VS, bf)
_sb("F PW", B0 + FN, bf)
_sb("TR", V + 256, bf)
_sb("WA WB", FB + FN, f32)
_sb("IOF", FN, f32)
_sb("SV", V, f32)
_sb("CIW", VS, f32)
_sb("CCP CC1 CC2 IDT", 4 * WS, bf)
_sb("CC3 CIH CH1 LHL", 2 * WS, bf)
_sb("MS MR", 2 * WS * TV, bf)
_sb("NS NR", W * TV, u16)
_sb("CIU CI1 CI2 CI3 LU CCU FOU", W, u16)
_sb("PLU YU", WF, u16)
_sb("PLI IA", WF, i32)
_sb("CCI NMI", W, i32)
_sb("IC ID", WS, i32)
_sb("FA FC FD TA TB ZT YT YL YO", WF, f32)
_sb("FE FG FH TAU DMP FV FP", W, f32)
_sb("CUM TC", WS, f32)
_sb("NH NL THR CMA CMB CMC GP GL KEEP KV", W, bf)
_sb("G1", 2 * W, bf)
_sb("FREE ZB", WS, bf)
_sb("IQ INV", WF, bf)
_sb("RC", WS + 16, bf)
_sb("EB", K * W, bf)
_sb("ZZ", 10 * 144, bf)
_sb("MM", 10 * 128, bf)
_sb("TD", 16 * 128, bf)
_sb("IM IDF", 128, f32)
_sb("PI", 16, i32)
_sb("CF", 32, f32)
_sb("CB", 16, bf)
_sb("SC", 16, f32)
_sb("KT", 16 * 10, f32)
_sb("KI", 16, i32)
_sb("KU", 16 * 10, u16)
_sb("BW", 16, f32)
PSUM = "J0 J1 J2 K0 K1 PV PD PL".split()
for _n in PSUM:
    SCRATCH[_n] = ("psum", [128, 512], f32)

ND = 100
ARR = ["ha", "hb", "hc", "ax0", "ax1", "ax2", "ax3", "ax4", "ac1", "ac2", "ac3", "ai1", "ai2", "ai3", "ah",
       "an1", "an2", "an3", "an4", "am1", "am2", "am3", "am4", "ay"]
SEMAPHORES = ["cv", "cs", "cp", "cg", "sent"] + ARR + ["d%d" % i for i in range(ND)]


ORDER = []
ROUNDS = 100
STEPS = 1200
SPAN = []


def order_calls(nodes):
    m = len(nodes)
    busy = [x["busy"] for x in nodes]
    lat = [x["lat"] for x in nodes]
    fwd = [[] for _ in range(m)]
    bwd = [[] for _ in range(m)]
    for k, x in enumerate(nodes):
        for j, w in x["pre"].items():
            lag = lat[j] + HOP if w else busy[j]
            fwd[j].append((k, lag))
            bwd[k].append((j, busy[k] + lag - busy[j]))

    def place(edges, first, prio):
        left = [0] * m
        for i in range(m):
            for k, _ in edges[i]:
                left[k] += 1
        ready = list(first)
        start = [0.0] * m
        taken = {}
        can = [i for i in range(m) if left[i] == 0]
        seq = []
        while can:
            i = min(can, key=lambda k: prio[k])
            can.remove(i)
            t0 = ready[i]
            q = nodes[i]["q"]
            if q is not None:
                spans = taken.setdefault(q, [])
                p = len(spans)
                while p > 0 and spans[p - 1][1] > t0:
                    p -= 1
                while p < len(spans) and spans[p][0] < t0 + busy[i] - 1e-9:
                    t0 = max(t0, spans[p][1])
                    p += 1
                spans.insert(p, (t0, t0 + busy[i]))
            start[i] = t0
            seq.append(i)
            for k, lag in edges[i]:
                ready[k] = max(ready[k], t0 + lag)
                left[k] -= 1
                if left[k] == 0:
                    can.append(k)
        return start, seq

    seed = [12345]

    def jitter(size):
        out = []
        for _ in range(m):
            seed[0] = (seed[0] * 1103515245 + 12345) % 2147483648
            out.append(size * seed[0] / 2147483648.0)
        return out

    best = None
    prio = [float(i) for i in range(m)]
    for r in range(ROUNDS):
        start, seq = place(fwd, [0.0] * m, prio)
        end = max(start[i] + lat[i] for i in range(m))
        if best is None or end < best[0]:
            best = (end, start, seq)
        base = best[1] if r % 4 == 3 else start
        noise = jitter(0.0 if r < 3 else (0.1, 0.3, 0.8)[r % 3])
        back, _ = place(bwd, [lat[i] - busy[i] for i in range(m)],
                        [float(noise[i]) - base[i] - busy[i] for i in range(m)])
        noise = jitter(0.0 if r < 3 else (0.05, 0.2, 0.5, 1.0, 0.0)[r % 5])
        prio = [float(noise[i]) - back[i] - busy[i] for i in range(m)]
    for r in range(STEPS):
        a = jitter(best[0])[0] - 4.0
        noise = jitter((0.3, 0.8, 2.0)[r % 3])
        prio = [best[1][i] + (noise[i] if a <= best[1][i] < a + 8.0 else 0.0) for i in range(m)]
        start, seq = place(fwd, [0.0] * m, prio)
        if r % 2:
            back, _ = place(bwd, [lat[i] - busy[i] for i in range(m)], [-start[i] - busy[i] for i in range(m)])
            start, seq = place(fwd, [0.0] * m, [-back[i] - busy[i] for i in range(m)])
        end = max(start[i] + lat[i] for i in range(m))
        if end <= best[0]:
            best = (end, start, seq)
    SPAN.append(best[0])
    where = {i: p for p, i in enumerate(best[2])}
    return sorted(range(m), key=lambda i: (best[1][i], where[i]))


def helper(T, topo, r):
    c, n = T.cores[r], len(T.cores)
    for h in topo.cores_of(c):
        if T.rank_of(h) is None and topo.die(h) != topo.die(c) and \
                all(topo.may_write(h, T.cores[(r - t) % n]) for t in range(1, TV + 1)):
            return h
    raise ValueError("no helper core")


def local_engines(T, topo, r):
    far = topo.engines(T.cores[r], T.cores[(r - 1) % len(T.cores)])
    return [e for e in topo.engines(T.cores[r], helper(T, topo, r)) if e not in far]


def write(g, T, topo, out, src, sem, dst, engines):
    mask = 0
    for e in engines:
        mask |= 1 << e
    rid, pid = topo.addr(dst)[0], topo.addr(dst)[1]
    g.remote_dma(out, src, T.sem[sem], T.sem.sent, pid, rid, mask)


def helper_program(g, core, r, T, topo):
    n = len(T.cores)
    m = len(local_engines(T, topo, r))
    sent = 0
    plan = [("hb", T.X1[:, V // 2:V], T.XO[:, V // 2:V], "ax1", 1), ("hc", T.CC1[:, :], T.CCP[:, :], "ac1", 1),
            ("ha", T.X2[:, :], T.XO[:, :], "ax2", 2), (None, T.CC2[:, :], T.CCP[:, :], "ac2", 2),
            (None, T.X3[:, :], T.XO[:, :], "ax3", 3), (None, T.CC3[:, :], T.CCP[:, 0:2 * WS], "ac3", 3),
            (None, T.X4[:, :], T.XO[:, :], "ax4", 4)]
    for need, out, src, sem, t in plan:
        if need:
            g.wait_ge(T.sem[need], m)
        dst = T.cores[(r - t) % n]
        e = topo.engines(core, dst)
        write(g, T, topo, out, src, sem, dst, e)
        sent += len(e)
    g.wait_ge(T.sem.sent, sent)


def rank_program(g, core, T, topo):
    rank = T.rank_of(core)
    n = len(T.cores)
    if rank is None:
        for r in range(n):
            if helper(T, topo, r) == core:
                helper_program(g, core, r, T, topo)
        return
    Q = {"v": g.vector, "s": g.scalar, "p": g.tensor, "g": g, "y": g.sync}
    CS = {"v": "cv", "s": "cs", "p": "cp", "g": "cg"}
    cnt = {}
    waited = {}
    hist = {}
    nd = [0]

    def A(b, lo=0, hi=None, st=1, parts=None):
        if hi is None:
            hi = SCRATCH[b][1][1]
        ps = slice(0, 128) if parts is None else slice(0, parts)
        ap = T[b][ps, lo:hi] if st == 1 else T[b][ps, lo:hi:st]
        return (b, ap, lo, hi, None)

    def ROW(b, r, lo, hi):
        return (b, T[b][r:128:16, lo:hi], lo, hi, r)

    def IND(win, off):
        return (win[0], win[1].indirect(off[1]), win[2], win[3], None, off)

    def col(b, j):
        return A(b, j, j + 1)

    def wait(q, tok):
        s, v = tok
        if waited.get((q, s), 0) < v:
            Q[q].wait_ge(T.sem[s], v)
            waited[(q, s)] = v

    nodes = []

    def node(q, kind, fn, reads, writes, busy, lat, cont=False):
        me = len(nodes)
        pre = {}
        for x, wr in [(r, False) for r in reads] + [(w, True) for w in writes]:
            b, lo, hi, row = x[0], x[2], x[3], x[4]
            ps = b in PSUM
            for (l2, h2, r2, w2, j) in hist.get(b, []):
                apart = h2 <= lo or hi <= l2 or (row is not None and r2 is not None and row != r2)
                same = kind == "c" and nodes[j]["kind"] == "c" and nodes[j]["q"] == q
                if same and q == "p" and ps:
                    pre[j] = pre.get(j, False) or (not apart and not cont)
                elif ((w2 or wr) and not apart) or (ps and not same):
                    pre[j] = True
        for x, wr in [(r, False) for r in reads] + [(w, True) for w in writes]:
            h = hist.setdefault(x[0], [])
            if wr and x[4] is None and not cont:
                h[:] = [e for e in h if not (x[2] <= e[0] and e[1] <= x[3] and e[4] in pre)]
            h.append((x[2], x[3], x[4], wr, me))
        nodes.append({"q": q, "kind": kind, "fn": fn, "pre": pre, "busy": busy, "lat": lat})
        return me

    def width(x):
        if len(x) > 5:
            return 16 * (x[5][3] - x[5][2])
        return x[3] - x[2]

    def cost(q, out, ins, per):
        ops = [x for x in ins if isinstance(x, tuple)]
        m = max(width(x) for x in [out] + ops[:1])
        if len(out) > 5:
            m, per = width(out), SCAT
        elif ops and len(ops[0]) > 5:
            m, per = width(out), GATH
        elif per is None:
            narrow = all(SCRATCH[x[0]][2] in (bf, u16) for x in [out] + ops if x[3] - x[2] > 1)
            per = 0.5 if narrow else 1.0
        return {"v": 0.05, "s": 0.065, "g": 0.15}[q] + max(64, m * per) * CYC

    def emit():
        tok = {}
        if not ORDER:
            ORDER.extend(order_calls(nodes))
        for i in ORDER:
            x = nodes[i]
            if x["kind"] == "arr":
                tok[i] = x["fn"]
                continue
            best = {}
            for j, w in x["pre"].items():
                if w:
                    s, v = tok[j]
                    best[s] = max(best.get(s, 0), v)
            for s, v in best.items():
                wait(x["q"], (s, v))
            ins = x["fn"]()
            if x["kind"] == "c":
                s = CS[x["q"]]
                cnt[s] = cnt.get(s, 0) + 1
                ins.then_inc(T.sem[s], 1)
                tok[i] = (s, cnt[s])
            elif x["kind"] == "dma":
                s = "d%d" % nd[0]
                nd[0] += 1
                cnt[s] = 16
                ins.then_inc(T.sem[s], 16)
                tok[i] = (s, 16)
        for s in sorted(cnt):
            wait("g", (s, cnt[s]))

    def split(ops):
        out = []
        for x in ops:
            if isinstance(x, tuple):
                out.append(x)
                if len(x) > 5:
                    out.append(x[5])
        return out

    def ap(x):
        return x[1] if isinstance(x, tuple) else x

    def run(q, fn, out, ins, per=None):
        reads = split(ins) + ([out[5]] if len(out) > 5 else [])
        d = cost(q, out, ins, per)
        node(q, "c", fn, reads, [out], d, d)

    def ts(out, in0, s1, op0, s2=None, op1=None):
        if op1 is None:
            run("v", lambda: g.vector.tensor_scalar(ap(out), ap(in0), ap(s1), None, op0), out, [in0, s1])
        else:
            run("v", lambda: g.vector.tensor_scalar(ap(out), ap(in0), ap(s1), ap(s2), op0, op1), out, [in0, s1, s2])

    def tt(out, a, b, op):
        run("v", lambda: g.vector.tensor_tensor(ap(out), ap(a), ap(b), op), out, [a, b],
            1.0 if a[0] in PSUM or b[0] in PSUM else 2.0)

    def cp(out, a):
        run("v", lambda: g.vector.tensor_copy(ap(out), ap(a)), out, [a])

    def fill(out, c):
        run("v", lambda: g.vector.memset(ap(out), c), out, [])

    def act(out, a, func=Act.Identity, bias=None, scale=None):
        kw = {}
        if bias is not None:
            kw["bias"] = ap(bias)
        if scale is not None:
            kw["scale"] = ap(scale)
        run("s", lambda: g.scalar.activation(ap(out), ap(a), func, **kw), out, [a, bias, scale], 1.0)

    def mm(out, terms, first=True, last=True):
        def fn():
            ins = None
            for i, x in enumerate(terms):
                o = x[2] if len(x) > 2 else out
                ins = g.tensor.matmul(o[1], x[0][1], x[1][1], first and i == 0, last and i == len(terms) - 1)
            return ins
        d = sum(max(64, x[1][1].shape[1]) * (4 if SCRATCH[x[0][0]][2] == f32 else 1) * PEC for x in terms)
        node("p", "c", fn, [y for x in terms for y in x[:2]], [out], d, d + 0.06, cont=not first)

    ZALL, Z16, ZWS, Z01, ZL, ZN0, Z45, Z67, Z89, ZAB = range(10)
    I1, I2, IN1, IN2, I256, INB, BO, TRI, BO45 = [A("MM", 128 * j, 128 * j + 128) for j in range(9)]
    IDF = A("IDF")

    def TDm(i):
        return A("TD", 128 * i, 128 * i + 128)

    def zs(z, i):
        return A("ZZ", 144 * z + 15 - i, 144 * z + 143 - i)

    def ext(out, b, lo, hi, z=ZALL, first=True, last=True):
        mm(out, [(zs(z, i), A(b, lo + i, hi, 16)) for i in range(16)], first, last)

    def dma(out, src, q="y", after=None):
        reads = ([src] if isinstance(src, tuple) else []) + ([after] if after else [])
        writes = [out] if isinstance(out, tuple) else []
        x = out if writes else src
        big = x[4] is None and x[3] - x[2] >= V
        node(q, "dma", lambda: Q[q].dma_start(ap(out), ap(src)), reads, writes, 0.07,
             (11.0 if SCRATCH[x[0]][2] == f32 else 6.0) if big else 2.3)

    def rows(win, r, b, lo, m=2):
        for j in range(m):
            dma(ROW(win, r + j, 0, VS), A(b, lo + j * WS, lo + (j + 1) * WS))

    arrival = {}

    def post(src, land, sem, dst, e, opens):
        cnt["sent"] = cnt.get("sent", 0) + len(e)
        i = node("g", "send", lambda: write(g, T, topo, land[1], src[1], sem, dst, e), [src], [], 0.3, 0.3)
        for s in opens:
            nodes[arrival[s]]["pre"][i] = True

    def send(src, land, sem, k):
        dst = T.cores[(rank + k) % n]
        post(src, land, sem, dst, topo.engines(core, dst), [sem])

    def hand(src, sem):
        opens = {"hb": ["ax1"], "hc": ["ac1", "ac2", "ac3"], "ha": ["ax2", "ax3", "ax4"]}[sem]
        post(src, src, sem, helper(T, topo, rank), local_engines(T, topo, rank), opens)

    def expect(land, sem, src):
        cnt[sem] = len(topo.engines(src, core))
        lat = {"ax0": 13.0, "ax1": 15.0, "ac1": 15.0, "ax2": 24.0, "ac2": 27.0, "ax3": 36.0, "ac3": 39.0, "ax4": 48.0,
               "ay": 4.5}.get(sem, 3.3)
        arrival[sem] = node(None, "arr", (sem, cnt[sem]), [], [land], lat, lat)

    def names(b, t):
        return A(b, W * t, W * t + W)

    def halves(b, t, h=None):
        if h is None:
            return A(b, 2 * WS * t, 2 * WS * (t + 1))
        return A(b, (2 * t + h) * WS, (2 * t + h) * WS + W)

    nxt = T.cores[(rank + 1) % n]
    for t in range(1, TV + 1):
        far = helper(T, topo, (rank + t) % n)
        if t == 1:
            expect(A("X1", 0, V // 2), "ax0", nxt)
            expect(A("X1", V // 2, V), "ax1", far)
        else:
            expect(A("X%d" % t), "ax%d" % t, far)
        expect(names("NR", t - 1), "an%d" % t, nxt)
        expect(halves("MR", t - 1), "am%d" % t, nxt)
        if t < TV:
            expect(A("CC%d" % t), "ac%d" % t, far)
            expect(A("CI%d" % t), "ai%d" % t, T.cores[(rank + t) % n])
    expect(A("CH1"), "ah", nxt)
    expect(A("YL"), "ay", T.cores[(rank - TV) % n])

    def iota(out, pat, base, cm):
        if SCRATCH[out[0]][2] == i32:
            run("g", lambda: g.iota(ap(out), pat, base, cm), out, [], 2.0)
        else:
            run("g", lambda: g.iota(ap(out), pat, base, cm, allow_small_or_imprecise_dtypes=True), out, [], 2.0)

    def pick(out, src, pat, base):
        run("g", lambda: g.affine_select(ap(out), ap(src), pat, Op.is_ge, 0.0, base, -1), out, [src], 2.0)

    def gather(q, out, win, off):
        if q == "v":
            cp(out, IND(win, off))
        else:
            act(out, IND(win, off))

    def scatter(q, win, off, lo, hi, vals, step):
        for a in range(lo, hi, step):
            b = min(hi, a + step)
            if q == "v":
                cp(IND(win, A(off, a, b)), A(vals, 16 * a, 16 * b))
            else:
                act(IND(win, A(off, a, b)), A(vals, 16 * a, 16 * b), Act.Silu)

    def pass_names(t, ps):
        cp(names("NS", t), ps)
        send(names("NS", t), names("NR", t), "an%d" % (t + 1), -1)
        act(halves("MS", t, 0), ps)
        tt(halves("MS", t, 1), ps, halves("MS", t, 0), Op.subtract)
        send(halves("MS", t), halves("MR", t), "am%d" % (t + 1), -1)

    PF, PM, PG, PH, ZC, R12, PW_, RL, R4, RD, RM = 0, 1, 2, 3, 4, 5, 6, 7, 16, 17, 8
    LH, LL = A("LHL", 0, W), A("LHL", WS, WS + W)

    def cf(j):
        return col("CF", j)

    def zmat(z, w=None):
        if w is None:
            ts(A("ZZ", 144 * z, 144 * z + 144), A("IQ", 0, 144), cf(ZC), Op.is_equal)
        else:
            ts(A("ZZ", 144 * z, 144 * z + 144), A("IQ", 0, 144), cf(ZC), Op.is_equal, w, Op.mult)

    def diag(out, w):
        ts(out, A("IQ", 0, 128), cf(PF), Op.is_equal, w, Op.mult)

    dma(A("CCI"), T.cc[:, :], "y")
    dma(A("PLI"), T.pl[:, :], "s")
    dma(A("NMI"), T.nm[:, :], "s")
    dma(A("XO"), T.tx[:, :], "y")
    iota(A("IOF", 0, 256), [[1, 256]], B0, 0)
    iota(col("PI", 0), [[1, 1]], 0, 1)
    iota(A("IQ"), [[1, WF]], 0, 0)
    for a, b in ((256, 512), (512, 1024), (1024, 2048), (2048, 3072), (3072, 4096)):
        act(A("IOF", a, b), A("IOF", 0, b - a), bias=float(a))
    for a in range(2):
        iota(A("SV", 1024 * a, 1024 * a + 1024), [[1, 64], [WS, 16]], BI + 64 * a, 0)
    fill(A("WL"), B0 / 2.0)
    fill(A("ZT"), 0.0)
    fill(A("CCP", 2 * WS, 4 * WS), 0.0)
    ts(col("PI", 1), col("PI", 0), 15, Op.bitwise_and)
    ts(col("PI", 2), col("PI", 0), 4, Op.arith_shift_right)
    ts(col("PI", 3), col("PI", 0), 15, Op.bitwise_and, 1, Op.arith_shift_right)
    cp(A("CF", 0, 4), A("PI", 0, 4))
    diag(I1, 1.0)
    for b in ("CIW", "WA", "WB"):
        dma(ROW(b, 0, 0, VS), A("ZT", 0, WS))

    ts(A("IC", 0, W), A("CCI"), 15, Op.bitwise_and)
    ts(A("ID", 0, W), A("CCI"), 4, Op.arith_shift_right)
    sh, sl = A("CCP", 2 * WS, 2 * WS + W), A("CCP", 3 * WS, 3 * WS + W)
    ts(sh, A("IC", 0, W), float(WS), Op.mult)
    cp(sl, A("ID", 0, W))
    rows("WL", 4, "CCP", 2 * WS)
    mm(A("K0", 0, W), [(I1, sh), (I1, sl)])
    cp(A("CCU"), A("K0", 0, W))
    act(A("CCP", 0, W), sl, scale=16.0)
    act(A("CCP", WS, WS + W), sh, scale=1.0 / WS)
    act(A("CCP", W, WS), A("IQ", W, WS), scale=16.0)
    act(A("CCP", WS + W, 2 * WS), A("ZT", 0, 16), bias=cf(PM))
    cp(A("NH"), A("NMI"))
    tt(A("NL"), A("NMI"), A("NH"), Op.subtract)
    dma(ROW("WL", 0, 0, V), A("NH"))
    dma(ROW("WL", 1, 0, V), A("NL"))
    hand(A("XO", V // 2, V), "hb")
    send(A("XO", 0, V // 2), A("X1", 0, V // 2), "ax0", -1)
    hand(A("CCP"), "hc")
    hand(A("XO", 0, V // 2), "ha")
    iota(A("SV", 2048, V), [[1, 64], [WS, 16]], BI + 128, 0)
    iota(A("FD"), [[0, WF // 64], [16, 64]], VS, 1)
    iota(A("IM"), [[1, 8], [0, 16]], 0, 0)
    scatter("s", A("CIW"), "CCU", 0, W, "SV", 32)
    ts(A("IA"), A("PLI"), 4, Op.arith_shift_right)
    ts(A("K1", 0, WF), A("PLI"), float(WS), Op.mult)
    ts(A("FC"), A("IA"), float(1 - VS), Op.mult)
    tt(A("FA"), A("K1", 0, WF), A("FC"), Op.add)
    cp(A("PLU"), A("FA"))
    ts(cf(ZC), cf(PG), 16.0, Op.mult, 15.0, Op.add)
    ts(A("CF", RM, RM + 8), A("IQ", 0, 8), cf(PH), Op.is_equal)
    ts(cf(R4), cf(PM), 4.0, Op.is_lt)
    zmat(Z45, cf(RM + 2))
    zmat(ZN0, cf(R4))
    ts(A("INV"), A("PLI"), 0.0, Op.is_lt, DEAD, Op.mult)
    fill(A("MS"), 0.0)
    dma(A("F", B0, B0 + FN), T.fo[:, :], "y", A("PLU"))
    dma(A("PW", 0, B0), T.fo[:, 0:B0], "y", A("PLU"))
    fill(A("F", 0, B0), 1024.0)
    ext(A("PV", 0, W), "WL", 0, V, ZN0)
    pass_names(0, A("PV", 0, W))
    for h in range(4):
        lo, hi = h * WF // 4, (h + 1) * WF // 4
        bank = A("J%d" % (h % 3), lo, hi)
        gather("v" if lo < YV else "s", A("PW", B0 + 16 * lo, B0 + 16 * hi), A("WL"), A("PLU", lo, hi))
        mm(bank, [(I1, A("INV", lo, hi))], last=False)
        ext(bank, "PW", B0 + 16 * lo, B0 + 16 * hi, Z45, first=False)
        tt(A("FA", lo, hi), bank, A("FD", lo, hi), Op.min)
        cp(A("YU", lo, hi), A("FA", lo, hi))
    scatter("v", A("WA"), "YU", 0, L1V, "IOF", 48)
    scatter("s", A("WB"), "YU", L1V, WF, "IOF", 56)
    dma(A("TA", 0, WS), ROW("WA", 0, 0, VS), "y")
    dma(A("TB", 0, WS), ROW("WB", 0, 0, VS), "s")
    dma(A("TC"), ROW("CIW", 0, 0, VS), "s")
    ts(A("CIU"), A("TC", 0, W), float(BI), Op.subtract)
    for t in (1, 2, 3):
        send(A("CIU"), A("CI%d" % t), "ai%d" % t, -t)
    ts(A("IC"), A("TC"), float(BI), Op.subtract, 0.0, Op.max)
    cp(A("CIH", 0, WS), A("IC"))
    tt(A("CIH", WS, 2 * WS), A("IC"), A("CIH", 0, WS), Op.subtract)
    send(A("CIH"), A("CH1"), "ah", -1)

    def kt(j):
        return A("KT", 16 * j, 16 * j + K)

    def ku(j):
        return A("KU", 16 * j, 16 * j + K)
    KW, KF, K1_, K2_, K3_, K4_ = [kt(j) for j in range(6)]
    diag(I2, 2.0)
    diag(IN2, -2.0)
    diag(IN1, -1.0)
    diag(IDF, 1.0)
    diag(I256, 256.0)
    diag(INB, -OUT)
    zmat(ZALL)
    zmat(Z16, 16.0)
    zmat(ZWS, float(WS))
    zmat(Z01, cf(RM))
    ts(cf(RD), cf(PM), 2.0, Op.is_equal, -DEAD, Op.mult)
    ts(cf(RL), cf(RD), cf(RM), Op.add)
    zmat(ZL, cf(RL))
    zmat(Z67, cf(RM + 3))
    zmat(Z89, cf(RM + 4))
    zmat(ZAB, cf(RM + 5))
    ts(BO, A("IM"), cf(PG), Op.is_equal)
    ts(BO45, A("IM"), cf(PG), Op.is_equal, cf(RM + 2), Op.mult)
    pick(TRI, BO, [[1, 128]], 0)
    for i in range(1, 16):
        pick(TDm(i), BO, [[16, 8], [0, 16]], i - 1)
    fill(A("ZB"), 0.0)
    fill(A("RC", 0, 1), 0.0)
    fill(A("FREE", W, WS), 1.0)
    fill(A("LHL"), 0.0)
    fill(A("CB"), -float(K))
    fill(A("YT"), 0.0)
    ts(cf(PW_), cf(PM), float(WS), Op.mult)
    ts(cf(R12), cf(PM), float(K), Op.is_lt)
    ts(KW, A("IQ", 0, K), 16.0, Op.mult, cf(PM), Op.add)
    ts(KF, KW, OUT - FB, Op.add)
    iota(A("DMP"), [[0, K], [16, 16]], 16 - FB, 1)
    act(A("IDT", 0, WS), A("ZB"), bias=cf(PW_))
    act(A("IDT", WS, 2 * WS), A("IQ", 0, WS))
    act(A("IDT", 2 * WS, 3 * WS), A("IQ", 0, WS), scale=16.0, bias=float(B0))
    act(A("IDT", 3 * WS, 4 * WS), A("ZB"), bias=cf(PM))
    dma(A("WN", 0, V), T.tx[:, :], "y", A("YU"))
    dma(A("WN", V, VS), T.tx[:, 0:VS - V], "y", A("YU"))
    dma(ROW("WN", 2, 0, VS), A("ZB"))

    tt(A("ID"), A("TA", 0, WS), A("TB", 0, WS), Op.add)
    cp(A("LU"), A("ID", 0, W))
    cp(LH, A("ID", 0, W))
    tt(LL, A("ID", 0, W), LH, Op.subtract)
    dma(A("WA", FB, FB + FN), A("IOF"), "y", A("LU"))
    for b in ("WA", "WB"):
        dma(ROW(b, 0, FB, FB + FN), A("ZT"))

    def rg(c):
        return c * CH, (c + 1) * CH

    def named(t):
        x = "X%d" % t
        for c in range(NCH):
            lo, hi = rg(c)
            off = A("NR", W * (t - 1) + lo // 16, W * (t - 1) + hi // 16)
            gather("v" if lo >= V - FNV else "s", A("FNB", lo, hi), A("F"), off)
            if KIND[c] == "E":
                mm(A("PV"), [(I1, A(x, lo, hi)), (IN1, A("FNB", lo, hi))])
                act(A("AQ", lo, hi), A("PV"), Act.Abs)

    def tables(t):
        rows("WL", 0, "LHL", 0)
        rows("WN", 0, "MR", 2 * WS * (t - 1))
        if t == 1:
            rows("WN", 4, "IDT", 0)
            rows("WN", 8, "CC1", 2 * WS)
        if t == 2:
            rows("WN", 4, "CH1", 0)
            rows("WN", 10, "CC2", 2 * WS)
        if t == TV:
            rows("WN", 4, "IDT", 2 * WS)
        else:
            rows("WN", 6, "CC%d" % t, 0)

    def judge(t):
        x = "X%d" % t
        mm(A("PL", 0, W), [(I1, halves("MR", t - 1, 0)), (I1, halves("MR", t - 1, 1)), (IN1, LH), (IN1, LL)])
        ts(A("THR"), A("PL", 0, W), 0.0, Op.is_equal, 100.0, Op.mult)
        tables(t)
        if t == TV:
            mm(A("PD", 0, W), [(I1, LH), (I1, LL)])
            ts(A("IC", 0, W), A("PD", 0, W), 1.0 / 16, Op.mult, -0.47, Op.add)
            ts(A("FE"), A("IC", 0, W), float(1 - FN), Op.mult)
            mm(A("PD", 0, W), [(I256, LH), (I256, LL), (IDF, A("FE"))], last=False)
        na, ne = 0, 0
        for c in range(NCH):
            r = rg(c)
            u = A("U", *r)
            listed = A("LU", r[0] // 16, r[1] // 16)
            if KIND[c] == "E":
                bank = A("K%d" % (ne % 2))
                ne += 1
                gather("s", u, A("F"), listed)
                mm(bank, [(I1, A(x, *r)), (IN1, u)])
                act(u, bank, Act.Abs)
                mm(bank, [(I1, u), (IN1, A("AQ", *r))])
                act(u, bank, Act.Sign, bias=0.5)
            else:
                bank = A("J%d" % (na % 3))
                na += 1
                mm(bank, [(IN2, A(x, *r)), (I2, A("FNB", *r))], last=False)
                tt(u, IND(A("F"), listed), A("FNB", *r), Op.subtract)
                mm(bank, [(I1, u)], first=False)
                tt(u, bank, u, Op.mult)
                if KIND[c] == "A":
                    ts(u, u, 0.0, Op.is_ge, 0.5, Op.subtract)
                else:
                    act(u, u, Act.Sign, bias=0.5)
            if c % 2:
                ext(A("PV", (c - 1) * CH // 16, (c + 1) * CH // 16), "U", (c - 1) * CH, (c + 1) * CH)

    def recount(t):
        s = (STEP * t) % V
        sc = s // 16
        last = t == TV
        g1 = A("G1", W * (t % 2), W * (t % 2) + W)
        g1r = (g1[2], g1[3])
        free = A("FREE", 0, W)
        tt(free, A("PV", 0, W), A("THR"), Op.is_ge)
        if not last:
            rows("WL", 2, "FREE", 0, 1)
        run("v", lambda: g.vector.tensor_tensor_scan(T.RC[:, 1:WS + 1], T.FREE[:, :], T.ZB[:, :], 0.0, Op.add, Op.add),
            A("RC", 1, WS + 1), [A("FREE"), A("ZB")])
        tot, cs = col("PV", 200), col("PV", 201)
        mm(tot, [(BO, col("RC", W)), (BO, col("CB", 0))])
        mm(cs, [(BO, col("RC", sc)), (TDm(s % 16), col("FREE", sc))])
        mm(col("K0", 16), [(zs(ZALL, i), col("RC", 16 * i + 16)) for i in range(K)])
        ext(A("J0", 0, K + 1), "RC", 1, WS + 1)
        mm(A("J0", 16, 16 + WS), [(BO, A("RC", 0, WS)), (TRI, A("FREE"))])
        act(A("BW", 0, K + 1), A("J0", 0, K + 1))
        act(A("CUM"), A("J0", 16, 16 + WS))
        mm(A("J2", 0, W), [(I1, A("ZB", 0, W))], last=False)
        if last:
            mm(A("PD", 0, W), [(INB, free)], first=False)
            tt(A("FG"), A("PD", 0, W), A("DMP"), Op.max)
            ts(A("FOU"), A("FG"), float(FB - 16), Op.add)
            scatter("s", A("WB"), "FOU", 0, FINS, "IOF", 16)
            scatter("v", A("WA"), "FOU", FINS, W, "IOF", 8)
        else:
            for lo in range(0, V - TRV, CH):
                hi = min(lo + CH, V - TRV)
                gather("s", A("TR", lo, hi), A("WL"), A("CI%d" % t, lo // 16, hi // 16))
            for lo in range(V - TRV, V, 256):
                gather("v", A("TR", lo, lo + 256), A("WL"), A("CI%d" % t, lo // 16, lo // 16 + 16))
        base = A("PV", 256, 256 + W)
        ts(col("SC", 0), tot, 0.0, Op.max, cs, Op.min)
        ts(col("SC", 1), col("SC", 0), -1.0, Op.mult, cs, Op.add)
        ts(base, A("IQ", 0, W), col("SC", 1), Op.is_ge, col("SC", 0), Op.mult)
        tt(A("TAU"), base, A("IQ", 0, W), Op.add)
        ts(A("CMA"), A("TAU"), col("K0", 16), Op.is_ge, cf(R12), Op.mult)
        pa, pb, pc = A("K0", 0, K), A("K1", 0, K), A("J1", 0, K)
        ext(pa, "CMA", 0, W)
        ext(pb, "CMA", 0, W, Z16, last=False)
        ext(pc, "CMA", 0, W, Z16, last=False)
        nb = A("J0" if last else "PD", 0, W)
        tt(A("FP"), A("PL", 0, W), free, Op.mult)
        mm(nb, [(I1, LH), (I1, LL), (IDF, A("FP"))])
        if not last:
            pass_names(t, nb)
        else:
            ts(A("FH"), nb, float(B0), Op.subtract)
        cp(ku(0), pa)
        tt(A("CMB"), IND(A("BW", 0, K + 1), ku(0)), A("TAU"), Op.is_le)
        ext(pb, "CMB", 0, W, first=False)
        ext(pc, "CMB", 0, W, first=False, last=False)
        cp(ku(1), pb)
        tt(A("CMC"), IND(A("CUM"), ku(1)), A("TAU"), Op.is_le)
        ext(pc, "CMC", 0, W, ZWS, first=False)
        cp(ku(2), pc)
        cp(g1, IND(A("WN"), ku(2)))
        ext(pa, "G1", g1r[0], g1r[1], Z01)
        mm(A("K1", 0, W), [(TDm(2), g1)])
        for j in range(K):
            ts(A("EB", W * j + 16 * j, W * j + W), A("K1", 16 * j, W), col("K0", j), Op.is_equal, -4.0, Op.mult)
            if j < K - 1:
                mm(A("J2", 16 * j + 16, W), [(BO, A("EB", W * j + 16 * j + 16, W * j + W))], False, False)
        mm(A("J2", 0, W), [(TDm(i), A("EB", i, WS * (K - 1) + i + 1, WS), A("J2", i, W, 16)) for i in range(1, 16)],
           False, False)
        if last:
            for gi in range(8):
                for h in range(2):
                    mm(A("J0", 32 * gi + 16 * h, 32 * gi + 16 * h + 16, parts=W // 2),
                       [(A("FH", h, W, 2), A("IDF", 16 * gi, 16 * gi + 16))])
            dma(A("TB"), ROW("WB", 0, FB, FB + FN), "s")
            act(A("YT", 0, WF, parts=W // 2), A("J0", 0, WF, parts=W // 2))
            send(A("YT"), A("YL"), "ay", TV)
            mm(A("PV", 0, W), [(BO45, g1)])
            cp(A("FV"), A("PV", 0, W))
            ts(A("KI", 0, K), pa, 1.0 / 16, Op.mult, -0.47, Op.add)
            ts(K1_, pa, float(WF), Op.mult, -16.0, Op.add)
            ts(K2_, A("KI", 0, K), float(FN - 1), Op.mult)
            tt(K3_, K1_, K2_, Op.subtract)
            cp(ku(3), K3_)
            mm(pc, [(IDF, K3_)], last=False)
            ts(A("GL"), IND(A("WA", FB, FB + FN), ku(3)), 1.0, Op.is_lt)
            mm(A("J2", 0, W), [(TDm(1), A("GL"))], first=False)
            ts(A("KEEP"), A("J2", 0, W), 0.5, Op.is_ge, OUT / 256, Op.mult)
            ext(pc, "KEEP", 0, W, Z16, first=False)
            tt(K4_, pc, KF, Op.max)
            ts(ku(4), K4_, FB - OUT, Op.add)
            cp(IND(A("WA"), ku(4)), A("FV"))
            dma(A("TA"), ROW("WA", 0, FB, FB + FN), "y")
            act(A("PL", 0, WF), A("TB"), scale=-32.0, bias=-float(B0))
            ts(A("IA"), A("TB"), float(B0), Op.subtract, -1.0, Op.max)
            tt(A("PL", WF, 2 * WF), A("PL", 0, WF), A("TA"), Op.add)
            tt(A("YO"), A("PL", WF, 2 * WF), A("IA"), Op.max)
            for gi in range(8):
                dma(T.yn[gi, :], A("YL", 32 * gi, 32 * gi + 32, parts=W // 2), "s")
            dma(T.yp[:, :], A("YO"), "y")
            return
        cp(ku(3), pa)
        cp(A("GP"), IND(A("PW"), ku(3)))
        ext(pc, "GP", 0, W, Z45)
        cp(ku(4), pc)
        ext(A("J0", 0, K), "G1", g1r[0], g1r[1], Z67)
        cp(ku(7), A("J0", 0, K))
        pos = ku(4)
        for v in range(1, t):
            cp(A("GP"), IND(A("WN"), pos))
            ext(pc, "GP", 0, W, (Z89, ZAB)[v - 1])
            pos = ku(4 + v)
            cp(pos, pc)
        named(t + 1)
        tt(A("GL"), IND(A("WL"), pos), g1, Op.not_equal)
        mm(A("J2", 0, W), [(TDm(3), A("GL"))], first=False)
        ts(A("KEEP"), A("J2", 0, W), 0.5, Op.is_ge)
        tt(IND(A("TR"), ku(7)), g1, A("KEEP"), Op.mult)
        ext(A("PL", 0, LQ), "TR", 0, 16 * LQ, ZL)
        ext(A("PD", 0, W), "TR", 0, V, ZL)
        cp(A("LU", 0, LQ), A("PL", 0, LQ))
        cp(A("LU", LQ, W), A("PD", LQ, W))
        act(LH, A("PD", 0, W))
        tt(LL, A("PD", 0, W), LH, Op.subtract)
        if t < 3:
            tt(A("KV"), g1, A("KEEP"), Op.mult)
            ext(A("PD", 0, K), "KV", 0, W, Z01)
            tt(K4_, A("PD", 0, K), KW, Op.max)
            cp(ku(8), K4_)
            cp(IND(A("PW"), ku(8)), g1)

    named(1)
    for t in range(1, TV + 1):
        judge(t)
        recount(t)
    emit()
